import numpy as np
import ml_dtypes


def mxq(x, axis, fmt="e4m3"):
    dtype, down = {"e4m3": (ml_dtypes.float8_e4m3fn, 7), "e5m2": (ml_dtypes.float8_e5m2, 14)}[fmt]
    v = np.moveaxis(np.asarray(x, np.float32).astype(ml_dtypes.bfloat16).astype(np.float64), axis, -1)
    blocks = v.reshape(v.shape[:-1] + (-1, 32))
    amax = np.abs(blocks).max(-1, keepdims=True)
    byte = np.maximum(np.where(amax > 0, np.frexp(amax)[1] - 1 + 127, 0) - down, 1)
    scale = np.exp2(byte - 127.0)
    codes = (blocks / scale).astype(np.float32).astype(dtype).astype(np.float64)
    return np.moveaxis((codes * scale).reshape(v.shape), -1, axis)


WIDE = False


def mx_kscale(k):
    if not WIDE:
        return np.ones(k)
    levels = np.array([10, -10, 5, -5, 0])
    if k % 512:
        return np.exp2(np.random.permutation(np.resize(levels, k // 32))).repeat(32)
    a = np.empty((k // 512, 16))
    for p in range(k // 512):
        a[p, :8] = np.random.permutation(np.resize(levels, 8))
        for g in range(8):
            far = levels[np.abs(levels - a[p, g]) >= 10]
            a[p, g + 8] = far[np.random.randint(len(far))]
    return np.exp2(a.ravel()).repeat(32)


def f64(x):
    return np.asarray(x).astype(np.float64)


def striped(idx):
    return np.tile(idx.reshape(-1, 16).T, (8, 1)).astype(np.uint16)


def unstriped(offs):
    return offs[:16].T.reshape(-1).astype(np.int64)


E2M1 = np.array([0.0, 0.5, 1.0, 1.5, 2.0, 3.0, 4.0, 6.0, -0.0, -0.5, -1.0, -1.5, -2.0, -3.0, -4.0, -6.0])


def pack_weight(w, fmt):
    k, n = w.shape
    w = f64(np.asarray(w, np.float32).astype(ml_dtypes.bfloat16)).reshape(k // 32, 32, n)
    amax = np.abs(w).max(1)
    if fmt == "e4m3":
        byte = np.frexp(amax)[1] - 1 + 127 - 7
    else:
        mant, ex = np.frexp(amax / 6.0)
        byte = np.where(mant > 0.5, ex, ex - 1) + 127
    byte = np.clip(np.where(amax > 0, byte, 1), 1, 254)
    scaled = (w * np.exp2(127.0 - byte)[:, None, :]).reshape(k, n).astype(np.float32)
    by_word = np.ascontiguousarray(scaled.reshape(k // 512, 128, 4, n).transpose(0, 1, 3, 2))
    if fmt == "e4m3":
        words = by_word.astype(ml_dtypes.float8_e4m3fn).view(np.uint8)
    else:
        c = by_word.astype(ml_dtypes.float4_e2m1fn).view(np.uint8) & 0xF
        words = (c[..., 0::2] | (c[..., 1::2] << 4)).reshape(k // 512, 128, 2 * n)
    return np.ascontiguousarray(words), np.ascontiguousarray(byte.astype(np.uint8).reshape(k // 512, 16, n))


def unpack_weight(words, scales, fmt):
    g, _, n = scales.shape
    words = np.ascontiguousarray(words).reshape(g, 128, n, -1)
    if fmt == "e4m3":
        vals = words.view(ml_dtypes.float8_e4m3fn).astype(np.float64)
    else:
        nib = np.empty((g, 128, n, 4), np.uint8)
        nib[..., 0::2] = words & 0xF
        nib[..., 1::2] = words >> 4
        vals = E2M1[nib]
    vals = vals * np.repeat(np.exp2(scales.astype(np.float64) - 127.0), 8, axis=1)[..., None]
    return vals.transpose(0, 1, 3, 2).reshape(g * 512, n)


def gelu(v):
    return 0.5 * v * (1.0 + np.tanh(np.sqrt(2.0 / np.pi) * (v + 0.044715 * v**3)))


K, H, N, T, S, P = 1024, 1024, 512, 2048, 1024, 512

def setup_inputs():
    n = np.random.standard_normal
    s = mx_kscale(K)[:, None]
    u = mx_kscale(H)[:, None]
    tab_words, tab_scales = pack_weight(n((K, T)) * s, "e4m3")
    w1_words, w1_scales = pack_weight(n((K, H)) / np.sqrt(K) / s, "e2m1")
    w4_words, w4_scales = pack_weight(1.5 * n((H, N)) / np.sqrt(H) / u, "e4m3")
    return {
        "tab_words": tab_words, "tab_scales": tab_scales,
        "offs": striped(np.random.permutation(T)[:S]),
        "pos1": striped(np.random.permutation(S)[:P]),
        "pos2": striped(np.random.permutation(S)[:P]),
        "pos3": striped(np.random.permutation(S)[:P]),
        "w1_words": w1_words, "w1_scales": w1_scales,
        "w2": (n((K, H)) / np.sqrt(K) / s * u.T).astype(np.float32),
        "w3": (1.5 * n((H, N)) / np.sqrt(H) / u).astype(np.float32),
        "w4_words": w4_words, "w4_scales": w4_scales,
        "house": n((N, P)).astype(np.float32),
    }

def reference(tab_words, tab_scales, offs, pos1, pos2, pos3, w1_words, w1_scales,
              w2, w3, w4_words, w4_scales, house):
    v = unpack_weight(tab_words, tab_scales, "e4m3")[:, unstriped(offs)]
    dish = unpack_weight(w1_words, w1_scales, "e2m1").T @ v
    bottle = mxq(f64(w2), 0, "e4m3").T @ v
    start = 1.0 / (1.0 + np.exp(-dish[:, unstriped(pos1)]))
    z = np.minimum(start, dish[:, unstriped(pos2)]) * bottle[:, unstriped(pos3)]
    zq = mxq(z, 0, "e4m3")
    e = mxq(f64(w3), 0, "e4m3").T @ zq
    d = unpack_weight(w4_words, w4_scales, "e4m3").T @ zq
    gate = 1.0 / (1.0 + np.exp(-e))
    return f64(house) + gate * d

@@ -1,0 +1,272 @@
+from contextlib import ExitStack
+
+import concourse.mybir as mybir
+
+K, H, N, T, S, M = 1024, 1024, 512, 2048, 1024, 512
+FLOPS = 2 * (2 * K * H * S + 2 * H * N * M)
+
+F32 = mybir.dt.float32
+BF16 = mybir.dt.bfloat16
+I32 = mybir.dt.int32
+U32 = mybir.dt.uint32
+U16 = mybir.dt.uint16
+U8 = mybir.dt.uint8
+FP8X4 = mybir.dt.float8_e4m3fn_x4
+FP4X4 = mybir.dt.float4_e2m1fn_x4
+ALU = mybir.AluOpType
+ACT = mybir.ActivationFunctionType
+
+P = 128
+PACK = 4
+PASS = P * PACK
+BANK = 512
+
+
+def tile_list_wine_pairing_menu_kernel(tc, tab_words, tab_scales, offs, pos1, pos2, pos3,
+                                                 w1_words, w1_scales, w2, w3, w4_words, w4_scales,
+                                                 house, out):
+    nc = tc.nc
+    with ExitStack() as ctx:
+        keep = ctx.enter_context(tc.tile_pool(name="keep", bufs=1))
+        work = ctx.enter_context(tc.tile_pool(name="work", bufs=1))
+        psum = ctx.enter_context(tc.psum_pool(name="psum", bufs=8))
+
+        def held(name, shape, dtype):
+            return keep.tile(shape, dtype, name=name, align_bytes=64)
+
+        offs_t = keep.tile([P, S // 16], U16, name="offs_t")
+        pos_t = [keep.tile([P, M // 16], U16, name="pos_t%d" % i) for i in range(3)]
+
+        tab_sc = held("tab_sc", [P, T], U8)
+        w1_sc_raw = held("w1_sc_raw", [P, H], U8)
+        v_sc_hi = held("v_sc_hi", [P, S], U8)
+        w1_sc_hi = held("w1_sc_hi", [P, H], U8)
+        w4_sc = held("w4_sc", [P, N], U8)
+        nc.gpsimd.memset(tab_sc[:].bitcast(I32), 0)
+        for plane in (w1_sc_raw, w4_sc, v_sc_hi, w1_sc_hi):
+            nc.vector.memset(plane[:].bitcast(I32), 0)
+        warm = held("warm", [P, 8], F32)
+        nc.vector.memset(warm[:, 0:4], 0.0)
+        nc.scalar.activation(out=warm[:, 4:8], in_=warm[:, 0:4], func=ACT.Sigmoid)
+
+        def load_scales(plane, scales):
+            for q in range(4):
+                nc.sync.dma_start(out=plane[32 * q: 32 * q + 8, :].bitcast(I32),
+                                  in_=scales[:, 4 * q: 4 * q + 4, :].bitcast(I32))
+
+        tab = [held("tab%d" % a, [P, T], I32) for a in range(2)]
+        w1_raw = [held("w1_raw%d" % b, [P, 2, 2 * BANK], U8) for b in range(2)]
+        w4 = held("w4", [P, 2, N], I32)
+        house_t = held("house_t", [P, 4, M], F32)
+        raw = {}
+
+        def load_tab(a):
+            nc.sync.dma_start(out=tab[a][:], in_=tab_words[a].rearrange("p t i -> p (t i)").bitcast(I32))
+
+        def load_rows(key):
+            if key[0] == "w2":
+                rows = w2[key[1] * PASS:(key[1] + 1) * PASS, key[2] * BANK:(key[2] + 1) * BANK]
+            else:
+                rows = w3[key[1] * PASS:(key[1] + 1) * PASS, :]
+            raw[key] = work.tile([P, PACK, BANK], F32, name="raw", bufs=4)
+            nc.sync.dma_start(out=raw[key][:], in_=rows.rearrange("(p j) c -> p j c", j=PACK))
+
+        def load_w1(b):
+            nc.sync.dma_start(out=w1_raw[b][:].bitcast(I32),
+                              in_=w1_words[:, :, 2 * b * BANK: 2 * (b + 1) * BANK].rearrange("a p c -> p a c").bitcast(I32))
+
+        def load_pos():
+            for i, pos in enumerate((pos1, pos2, pos3)):
+                nc.sync.dma_start(pos_t[i][:], pos)
+
+        def load_tail():
+            for q in range(4):
+                nc.sync.dma_start(out=w4_sc[32 * q: 32 * q + 8, :].bitcast(I32),
+                                  in_=w4_scales[:, 4 * q: 4 * q + 4, :].bitcast(I32))
+            for a in range(2):
+                load_rows(("w3", a))
+            nc.sync.dma_start(out=w4[:], in_=w4_words.rearrange("a p c i -> p a (c i)").bitcast(I32))
+            nc.sync.dma_start(out=house_t[:], in_=house.rearrange("(j p) m -> p j m", p=P))
+
+        nc.sync.dma_start(offs_t[:], offs)
+        load_tab(0)
+        load_scales(tab_sc, tab_scales)
+        load_rows(("w2", 0, 0))
+        load_tab(1)
+        load_scales(w1_sc_raw, w1_scales)
+        load_w1(0)
+
+        v = [held("v%d" % a, [P, S], U32) for a in range(2)]
+        v_sc = held("v_sc", [P, S], U8)
+        w1_sc = held("w1_sc", [P, H], U8)
+        w1 = [held("w1_%d" % b, [P, 2, 2 * BANK], U8) for b in range(2)]
+
+        def gather_words(a):
+            nc.vector.tensor_copy(out=v[a][:], in_=tab[a][:].bitcast(U32).indirect(offs_t[:]))
+
+        def lift(dst, src):
+            nc.sync.dma_start(out=dst[0:100, :].bitcast(I32), in_=src[4:104, :].bitcast(I32))
+
+        def gather_scales():
+            nc.vector.tensor_copy(out=v_sc[:], in_=tab_sc[:].indirect(offs_t[:]))
+            lift(v_sc_hi, v_sc)
+
+        def order_w1_scales():
+            nc.vector.tensor_copy(
+                out=w1_sc[:].rearrange("p (b t c i) -> p b c t i", b=2, t=PACK, i=16),
+                in_=w1_sc_raw[:].rearrange("p (b c i t) -> p b c t i", b=2, t=PACK, i=16))
+            lift(w1_sc_hi, w1_sc)
+
+        def order_w1(b):
+            nc.vector.tensor_copy(
+                out=w1[b][:].bitcast(U16).rearrange("p a (t c i) -> p a c t i", t=PACK, i=8),
+                in_=w1_raw[b][:].bitcast(U16).rearrange("p a (c i t) -> p a c t i", t=PACK, i=8))
+
+        codes, scales, woven = {}, {}, {}
+
+        def pool_copy(out, in_):
+            nc.gpsimd.tensor_scalar(out=out, in0=in_, scalar1=1.0, scalar2=0.0, op0=ALU.mult, op1=ALU.add)
+
+        def weave(key, part, parts, engine):
+            if key not in woven:
+                woven[key] = work.tile([P, PACK * BANK], BF16, name="woven", bufs=3, align_bytes=64)
+            copy = {"v": nc.vector.tensor_copy, "s": nc.scalar.copy, "g": pool_copy}[engine]
+            cols = slice(part * P // parts, (part + 1) * P // parts)
+            if key[0] == "w2":
+                copy(out=woven[key][:].rearrange("p (t m j) -> p m j t", t=PACK, j=PACK)[:, cols],
+                     in_=raw[key][:].rearrange("p j (m t) -> p m j t", t=PACK)[:, cols])
+            else:
+                copy(out=woven[key][:].rearrange("p (m i j) -> p m j i", i=PACK, j=PACK)[:, cols],
+                     in_=raw[key][:].rearrange("p j (m i) -> p m j i", i=PACK)[:, cols])
+
+        def quantize(key):
+            name = "_".join(str(x) for x in key)
+            codes[key] = held("codes_" + name, [P, BANK], U32)
+            scales[key] = held("scales_" + name, [P, BANK], U8)
+            nc.vector.quantize_mx(out=codes[key][:].bitcast(FP8X4), scales=scales[key][:], in_=woven[key][:])
+
+        def weave_quantize(key, engines):
+            for part in range(len(engines)):
+                weave(key, part, len(engines), engines[part])
+            quantize(key)
+
+        low = [work.tile([P, PACK, M], F32, name="low%d" % b) for b in range(2)]
+        picked = [work.tile([P, PACK, M], F32, name="picked%d" % b) for b in range(2)]
+
+        def dish(b, t):
+            rows = work.tile([P, S], F32, name="dish_rows", bufs=4)
+            cols = slice(t * P, (t + 1) * P)
+            for h in range(2):
+                acc = psum.tile([P, BANK], F32, name="acc")
+                hc = slice(h * BANK, (h + 1) * BANK)
+                for a in range(2):
+                    nc.tensor.matmul_mx(
+                        out=acc[:], lhsT=w1[b][:, a, 2 * t * P: 2 * (t + 1) * P].bitcast(FP4X4),
+                        lhsT_scale=(w1_sc, w1_sc_hi)[a][:, b * BANK + t * P: b * BANK + (t + 1) * P],
+                        rhs=v[a][:, hc].bitcast(FP8X4), rhs_scale=(v_sc, v_sc_hi)[a][:, hc],
+                        start=(a == 0), stop=(a == 1))
+                nc.scalar.copy(out=rows[:, hc], in_=acc[:])
+            nc.scalar.activation(out=low[b][:, t, :], in_=rows[:].indirect(pos_t[0][:]), func=ACT.Sigmoid)
+            main = work.tile([P, M], F32, name="main", bufs=2)
+            nc.vector.tensor_copy(out=main[:], in_=rows[:].indirect(pos_t[1][:]))
+            return main
+
+        def lower(b, t, main):
+            nc.vector.tensor_tensor(out=low[b][:, t, :], in0=low[b][:, t, :], in1=main[:], op=ALU.min)
+
+        def bottle(b, t):
+            rows = work.tile([P, S], F32, name="bottle_rows", bufs=4)
+            cols = slice(t * P, (t + 1) * P)
+            for h in range(2):
+                acc = psum.tile([P, BANK], F32, name="acc")
+                hc = slice(h * BANK, (h + 1) * BANK)
+                for a in range(2):
+                    nc.tensor.matmul_mx(
+                        out=acc[:], lhsT=codes[("w2", a, b)][:, cols].bitcast(FP8X4),
+                        lhsT_scale=scales[("w2", a, b)][:, cols],
+                        rhs=v[a][:, hc].bitcast(FP8X4), rhs_scale=v_sc[4 * a:, hc],
+                        start=(a == 0), stop=(a == 1))
+                nc.scalar.copy(out=rows[:, hc], in_=acc[:])
+            nc.vector.tensor_tensor(out=picked[b][:, t, :], in0=rows[:].indirect(pos_t[2][:]), in1=low[b][:, t, :], op=ALU.mult)
+
+        HALF = M // 2
+        z_codes = {}
+        z_scales = {}
+        z_woven = {}
+
+        def combine(b, h):
+            z_woven[b, h] = work.tile([P, PACK * HALF], BF16, name="z_woven", bufs=2, align_bytes=64)
+            cols = slice(h * HALF, (h + 1) * HALF)
+            nc.vector.tensor_copy(out=z_woven[b, h][:].rearrange("p (c i t) -> p c t i", i=4, t=PACK),
+                                  in_=picked[b][:, :, cols].rearrange("p t (c i) -> p c t i", i=4))
+
+        def quantize_z(b, h):
+            z_codes[b, h] = held("z_codes%d_%d" % (b, h), [P, HALF], U32)
+            z_scales[b, h] = held("z_scales%d_%d" % (b, h), [P, HALF], U8)
+            nc.vector.quantize_mx(out=z_codes[b, h][:].bitcast(FP8X4), scales=z_scales[b, h][:], in_=z_woven[b, h][:])
+
+        def second_stage(j, h):
+            acc = psum.tile([P, 2, HALF], F32, name="acc")
+            cols = slice(j * P, (j + 1) * P)
+            for a in range(2):
+                nc.tensor.matmul_mx(out=acc[:, 0, :], lhsT=codes[("w3", a)][:, cols].bitcast(FP8X4),
+                                    lhsT_scale=scales[("w3", a)][:, cols], rhs=z_codes[a, h][:].bitcast(FP8X4),
+                                    rhs_scale=z_scales[a, h][:], start=(a == 0), stop=(a == 1))
+            for a in range(2):
+                nc.tensor.matmul_mx(out=acc[:, 1, :], lhsT=w4[:, a, cols].bitcast(FP8X4),
+                                    lhsT_scale=w4_sc[4 * a:, cols], rhs=z_codes[a, h][:].bitcast(FP8X4),
+                                    rhs_scale=z_scales[a, h][:], start=(a == 0), stop=(a == 1))
+            gate = work.tile([P, HALF], F32, name="gate", bufs=8)
+            nc.scalar.activation(out=gate[:], in_=acc[:, 0, :], func=ACT.Sigmoid)
+            nc.vector.tensor_tensor(out=gate[:], in0=acc[:, 1, :], in1=gate[:], op=ALU.mult)
+            return gate
+
+        def finish(j, h, change, engine):
+            cols = slice(h * HALF, (h + 1) * HALF)
+            engine.tensor_tensor(out=change[:], in0=change[:], in1=house_t[:, j, cols], op=ALU.add)
+            nc.sync.dma_start(out=out[j * P:(j + 1) * P, cols], in_=change[:])
+
+        gather_scales()
+        gather_words(0)
+        order_w1_scales()
+        load_rows(("w2", 1, 0))
+        load_pos()
+        load_rows(("w2", 0, 1))
+        load_rows(("w2", 1, 1))
+        load_w1(1)
+        load_tail()
+        gather_words(1)
+        order_w1(0)
+        weave_quantize(("w2", 0, 0), "ss")
+        weave_quantize(("w2", 1, 0), "ss")
+        lower(0, 0, dish(0, 0))
+        lower(0, 1, dish(0, 1))
+        order_w1(1)
+        for i in range(8):
+            b, t = divmod(i, 4)
+            bottle(b, t)
+            if i + 2 < 8:
+                nb, nt = divmod(i + 2, 4)
+                lower(nb, nt, dish(nb, nt))
+            if i < 2:
+                weave_quantize(("w2", i, 1), "ss")
+            if i == 3:
+                combine(0, 0)
+                combine(0, 1)
+            if i == 4:
+                quantize_z(0, 0)
+                quantize_z(0, 1)
+            if i in (4, 5):
+                weave_quantize(("w3", i - 4), "vv")
+        combine(1, 0)
+        combine(1, 1)
+        quantize_z(1, 0)
+        quantize_z(1, 1)
+        steps = [(j, h) for h in range(2) for j in range(4)]
+        last = None
+        for i, (j, h) in enumerate(steps):
+            change = second_stage(j, h)
+            if last is not None:
+                finish(*last)
+            last = (j, h, change, nc.vector)
+        finish(*last)

@@ -38,12 +38,11 @@ def tile_list_wine_pairing_menu_kernel(tc, tab_words, tab_scales, offs, pos1, po
         pos_t = [keep.tile([P, M // 16], U16, name="pos_t%d" % i) for i in range(3)]
 
         tab_sc = held("tab_sc", [P, T], U8)
-        w1_sc_raw = held("w1_sc_raw", [P, H], U8)
+        w1_sc_raw = held("w1_sc_raw", [P, 2, H], U8)
         v_sc_hi = held("v_sc_hi", [P, S], U8)
-        w1_sc_hi = held("w1_sc_hi", [P, H], U8)
         w4_sc = held("w4_sc", [P, N], U8)
         nc.gpsimd.memset(tab_sc[:].bitcast(I32), 0)
-        for plane in (w1_sc_raw, w4_sc, v_sc_hi, w1_sc_hi):
+        for plane in (w1_sc_raw, w4_sc, v_sc_hi):
             nc.vector.memset(plane[:].bitcast(I32), 0)
         warm = held("warm", [P, 8], F32)
         nc.vector.memset(warm[:, 0:4], 0.0)
@@ -53,6 +52,11 @@ def tile_list_wine_pairing_menu_kernel(tc, tab_words, tab_scales, offs, pos1, po
             for q in range(4):
                 nc.sync.dma_start(out=plane[32 * q: 32 * q + 8, :].bitcast(I32),
                                   in_=scales[:, 4 * q: 4 * q + 4, :].bitcast(I32))
+
+        def load_w1_scales(queue):
+            for q in range(4):
+                queue.dma_start(out=w1_sc_raw[32 * q: 32 * q + 4, :, :].bitcast(I32),
+                                in_=w1_scales[:, 4 * q: 4 * q + 4, :].rearrange("a r c -> r a c").bitcast(I32))
 
         tab = [held("tab%d" % a, [P, T], I32) for a in range(2)]
         w1_raw = [held("w1_raw%d" % b, [P, 2, 2 * BANK], U8) for b in range(2)]
@@ -80,25 +84,23 @@ def tile_list_wine_pairing_menu_kernel(tc, tab_words, tab_scales, offs, pos1, po
                 nc.sync.dma_start(pos_t[i][:], pos)
 
         def load_tail():
-            for q in range(4):
-                nc.sync.dma_start(out=w4_sc[32 * q: 32 * q + 8, :].bitcast(I32),
-                                  in_=w4_scales[:, 4 * q: 4 * q + 4, :].bitcast(I32))
             for a in range(2):
                 load_rows(("w3", a))
+            load_scales(w4_sc, w4_scales)
             nc.sync.dma_start(out=w4[:], in_=w4_words.rearrange("a p c i -> p a (c i)").bitcast(I32))
             nc.sync.dma_start(out=house_t[:], in_=house.rearrange("(j p) m -> p j m", p=P))
 
         nc.sync.dma_start(offs_t[:], offs)
-        load_tab(0)
         load_scales(tab_sc, tab_scales)
-        load_rows(("w2", 0, 0))
+        load_tab(0)
         load_tab(1)
-        load_scales(w1_sc_raw, w1_scales)
         load_w1(0)
+        load_w1_scales(nc.sync)
+        load_rows(("w2", 0, 0))
 
         v = [held("v%d" % a, [P, S], U32) for a in range(2)]
         v_sc = held("v_sc", [P, S], U8)
-        w1_sc = held("w1_sc", [P, H], U8)
+        w1_sc = [held("w1_sc%d" % b, [P, 2, BANK], U8) for b in range(2)]
         w1 = [held("w1_%d" % b, [P, 2, 2 * BANK], U8) for b in range(2)]
 
         def gather_words(a):
@@ -111,11 +113,10 @@ def tile_list_wine_pairing_menu_kernel(tc, tab_words, tab_scales, offs, pos1, po
             nc.vector.tensor_copy(out=v_sc[:], in_=tab_sc[:].indirect(offs_t[:]))
             lift(v_sc_hi, v_sc)
 
-        def order_w1_scales():
+        def order_w1_scales(b):
             nc.vector.tensor_copy(
-                out=w1_sc[:].rearrange("p (b t c i) -> p b c t i", b=2, t=PACK, i=16),
-                in_=w1_sc_raw[:].rearrange("p (b c i t) -> p b c t i", b=2, t=PACK, i=16))
-            lift(w1_sc_hi, w1_sc)
+                out=w1_sc[b][:].rearrange("p a (t c i) -> p a c t i", t=PACK, i=16),
+                in_=w1_sc_raw[:, :, b * BANK:(b + 1) * BANK].rearrange("p a (c i t) -> p a c t i", t=PACK, i=16))
 
         def order_w1(b):
             nc.vector.tensor_copy(
@@ -153,19 +154,25 @@ def tile_list_wine_pairing_menu_kernel(tc, tab_words, tab_scales, offs, pos1, po
         low = [work.tile([P, PACK, M], F32, name="low%d" % b) for b in range(2)]
         picked = [work.tile([P, PACK, M], F32, name="picked%d" % b) for b in range(2)]
 
+        def empty(key, dst, acc):
+            if key in ():
+                nc.vector.tensor_copy(out=dst, in_=acc)
+            else:
+                nc.scalar.copy(out=dst, in_=acc)
+
         def dish(b, t):
             rows = work.tile([P, S], F32, name="dish_rows", bufs=4)
             cols = slice(t * P, (t + 1) * P)
             for h in range(2):
                 acc = psum.tile([P, BANK], F32, name="acc")
                 hc = slice(h * BANK, (h + 1) * BANK)
-                for a in range(2):
+                for a in (1, 0):
                     nc.tensor.matmul_mx(
                         out=acc[:], lhsT=w1[b][:, a, 2 * t * P: 2 * (t + 1) * P].bitcast(FP4X4),
-                        lhsT_scale=(w1_sc, w1_sc_hi)[a][:, b * BANK + t * P: b * BANK + (t + 1) * P],
+                        lhsT_scale=w1_sc[b][:, a, cols],
                         rhs=v[a][:, hc].bitcast(FP8X4), rhs_scale=(v_sc, v_sc_hi)[a][:, hc],
-                        start=(a == 0), stop=(a == 1))
-                nc.scalar.copy(out=rows[:, hc], in_=acc[:])
+                        start=(a == 1), stop=(a == 0))
+                empty(("d", 4 * b + t, h), rows[:, hc], acc[:])
             nc.scalar.activation(out=low[b][:, t, :], in_=rows[:].indirect(pos_t[0][:]), func=ACT.Sigmoid)
             main = work.tile([P, M], F32, name="main", bufs=2)
             nc.vector.tensor_copy(out=main[:], in_=rows[:].indirect(pos_t[1][:]))
@@ -186,8 +193,8 @@ def tile_list_wine_pairing_menu_kernel(tc, tab_words, tab_scales, offs, pos1, po
                         lhsT_scale=scales[("w2", a, b)][:, cols],
                         rhs=v[a][:, hc].bitcast(FP8X4), rhs_scale=v_sc[4 * a:, hc],
                         start=(a == 0), stop=(a == 1))
-                nc.scalar.copy(out=rows[:, hc], in_=acc[:])
-            nc.vector.tensor_tensor(out=picked[b][:, t, :], in0=rows[:].indirect(pos_t[2][:]), in1=low[b][:, t, :], op=ALU.mult)
+                empty(("b", 4 * b + t, h), rows[:, hc], acc[:])
+            nc.vector.tensor_copy(out=picked[b][:, t, :], in_=rows[:].indirect(pos_t[2][:]))
 
         HALF = M // 2
         z_codes = {}
@@ -197,8 +204,9 @@ def tile_list_wine_pairing_menu_kernel(tc, tab_words, tab_scales, offs, pos1, po
         def combine(b, h):
             z_woven[b, h] = work.tile([P, PACK * HALF], BF16, name="z_woven", bufs=2, align_bytes=64)
             cols = slice(h * HALF, (h + 1) * HALF)
-            nc.vector.tensor_copy(out=z_woven[b, h][:].rearrange("p (c i t) -> p c t i", i=4, t=PACK),
-                                  in_=picked[b][:, :, cols].rearrange("p t (c i) -> p c t i", i=4))
+            nc.vector.tensor_tensor(out=z_woven[b, h][:].rearrange("p (c i t) -> p c t i", i=4, t=PACK),
+                                    in0=low[b][:, :, cols].rearrange("p t (c i) -> p c t i", i=4),
+                                    in1=picked[b][:, :, cols].rearrange("p t (c i) -> p c t i", i=4), op=ALU.mult)
 
         def quantize_z(b, h):
             z_codes[b, h] = held("z_codes%d_%d" % (b, h), [P, HALF], U32)
@@ -228,7 +236,6 @@ def tile_list_wine_pairing_menu_kernel(tc, tab_words, tab_scales, offs, pos1, po
 
         gather_scales()
         gather_words(0)
-        order_w1_scales()
         load_rows(("w2", 1, 0))
         load_pos()
         load_rows(("w2", 0, 1))
@@ -236,11 +243,13 @@ def tile_list_wine_pairing_menu_kernel(tc, tab_words, tab_scales, offs, pos1, po
         load_w1(1)
         load_tail()
         gather_words(1)
+        order_w1_scales(0)
         order_w1(0)
-        weave_quantize(("w2", 0, 0), "ss")
-        weave_quantize(("w2", 1, 0), "ss")
         lower(0, 0, dish(0, 0))
+        weave_quantize(("w2", 0, 0), "sv")
+        weave_quantize(("w2", 1, 0), "vv")
         lower(0, 1, dish(0, 1))
+        order_w1_scales(1)
         order_w1(1)
         for i in range(8):
             b, t = divmod(i, 4)
@@ -248,16 +257,18 @@ def tile_list_wine_pairing_menu_kernel(tc, tab_words, tab_scales, offs, pos1, po
             if i + 2 < 8:
                 nb, nt = divmod(i + 2, 4)
                 lower(nb, nt, dish(nb, nt))
-            if i < 2:
-                weave_quantize(("w2", i, 1), "ss")
+            if i in (1, 2):
+                weave_quantize(("w2", (1, 2).index(i), 1), "sv")
             if i == 3:
                 combine(0, 0)
                 combine(0, 1)
             if i == 4:
                 quantize_z(0, 0)
                 quantize_z(0, 1)
-            if i in (4, 5):
-                weave_quantize(("w3", i - 4), "vv")
+            if i in ():
+                weave_quantize(("w3", ().index(i)), "ss")
+        for a in range(2):
+            weave_quantize(("w3", a), "ss")
         combine(1, 0)
         combine(1, 1)
         quantize_z(1, 0)

@@ -40,10 +40,13 @@ def tile_list_wine_pairing_menu_kernel(tc, tab_words, tab_scales, offs, pos1, po
         tab_sc = held("tab_sc", [P, T], U8)
         w1_sc_raw = held("w1_sc_raw", [P, 2, H], U8)
         v_sc_hi = held("v_sc_hi", [P, S], U8)
+        v_sc_lo = held("v_sc_lo", [P, S], U8)
         w4_sc = held("w4_sc", [P, N], U8)
-        nc.gpsimd.memset(tab_sc[:].bitcast(I32), 0)
-        for plane in (w1_sc_raw, w4_sc, v_sc_hi):
-            nc.vector.memset(plane[:].bitcast(I32), 0)
+        for q in range(4):
+            nc.vector.memset(tab_sc[32 * q: 32 * q + 24, :].bitcast(I32), 0)
+        nc.vector.memset(w1_sc_raw[:].bitcast(I32), 0)
+        for plane in (v_sc_lo, v_sc_hi, w4_sc):
+            nc.gpsimd.memset(plane[:].bitcast(I32), 0)
         warm = held("warm", [P, 8], F32)
         nc.vector.memset(warm[:, 0:4], 0.0)
         nc.scalar.activation(out=warm[:, 4:8], in_=warm[:, 0:4], func=ACT.Sigmoid)
@@ -57,6 +60,11 @@ def tile_list_wine_pairing_menu_kernel(tc, tab_words, tab_scales, offs, pos1, po
             for q in range(4):
                 queue.dma_start(out=w1_sc_raw[32 * q: 32 * q + 4, :, :].bitcast(I32),
                                 in_=w1_scales[:, 4 * q: 4 * q + 4, :].rearrange("a r c -> r a c").bitcast(I32))
+
+        def load_tab_scales():
+            for q in range(4):
+                nc.sync.dma_start(out=tab_sc[32 * q + 24: 32 * q + 32, :].bitcast(I32),
+                                  in_=tab_scales[:, 4 * q: 4 * q + 4, :].bitcast(I32))
 
         tab = [held("tab%d" % a, [P, T], I32) for a in range(2)]
         w1_raw = [held("w1_raw%d" % b, [P, 2, 2 * BANK], U8) for b in range(2)]
@@ -79,9 +87,8 @@ def tile_list_wine_pairing_menu_kernel(tc, tab_words, tab_scales, offs, pos1, po
             nc.sync.dma_start(out=w1_raw[b][:].bitcast(I32),
                               in_=w1_words[:, :, 2 * b * BANK: 2 * (b + 1) * BANK].rearrange("a p c -> p a c").bitcast(I32))
 
-        def load_pos():
-            for i, pos in enumerate((pos1, pos2, pos3)):
-                nc.sync.dma_start(pos_t[i][:], pos)
+        def load_pos(i):
+            nc.sync.dma_start(pos_t[i][:], (pos1, pos2, pos3)[i])
 
         def load_tail():
             for a in range(2):
@@ -91,12 +98,11 @@ def tile_list_wine_pairing_menu_kernel(tc, tab_words, tab_scales, offs, pos1, po
             nc.sync.dma_start(out=house_t[:], in_=house.rearrange("(j p) m -> p j m", p=P))
 
         nc.sync.dma_start(offs_t[:], offs)
-        load_scales(tab_sc, tab_scales)
+        load_tab_scales()
         load_tab(0)
         load_tab(1)
         load_w1(0)
         load_w1_scales(nc.sync)
-        load_rows(("w2", 0, 0))
 
         v = [held("v%d" % a, [P, S], U32) for a in range(2)]
         v_sc = held("v_sc", [P, S], U8)
@@ -106,12 +112,13 @@ def tile_list_wine_pairing_menu_kernel(tc, tab_words, tab_scales, offs, pos1, po
         def gather_words(a):
             nc.vector.tensor_copy(out=v[a][:], in_=tab[a][:].bitcast(U32).indirect(offs_t[:]))
 
-        def lift(dst, src):
-            nc.sync.dma_start(out=dst[0:100, :].bitcast(I32), in_=src[4:104, :].bitcast(I32))
+        def lift(dst, src, by=4):
+            nc.sync.dma_start(out=dst[0:100, :].bitcast(I32), in_=src[by:by + 100, :].bitcast(I32))
 
         def gather_scales():
             nc.vector.tensor_copy(out=v_sc[:], in_=tab_sc[:].indirect(offs_t[:]))
-            lift(v_sc_hi, v_sc)
+            lift(v_sc_lo, v_sc, 24)
+            lift(v_sc_hi, v_sc, 28)
 
         def order_w1_scales(b):
             nc.vector.tensor_copy(
@@ -170,7 +177,7 @@ def tile_list_wine_pairing_menu_kernel(tc, tab_words, tab_scales, offs, pos1, po
                     nc.tensor.matmul_mx(
                         out=acc[:], lhsT=w1[b][:, a, 2 * t * P: 2 * (t + 1) * P].bitcast(FP4X4),
                         lhsT_scale=w1_sc[b][:, a, cols],
-                        rhs=v[a][:, hc].bitcast(FP8X4), rhs_scale=(v_sc, v_sc_hi)[a][:, hc],
+                        rhs=v[a][:, hc].bitcast(FP8X4), rhs_scale=(v_sc_lo, v_sc_hi)[a][:, hc],
                         start=(a == 1), stop=(a == 0))
                 empty(("d", 4 * b + t, h), rows[:, hc], acc[:])
             nc.scalar.activation(out=low[b][:, t, :], in_=rows[:].indirect(pos_t[0][:]), func=ACT.Sigmoid)
@@ -191,10 +198,10 @@ def tile_list_wine_pairing_menu_kernel(tc, tab_words, tab_scales, offs, pos1, po
                     nc.tensor.matmul_mx(
                         out=acc[:], lhsT=codes[("w2", a, b)][:, cols].bitcast(FP8X4),
                         lhsT_scale=scales[("w2", a, b)][:, cols],
-                        rhs=v[a][:, hc].bitcast(FP8X4), rhs_scale=v_sc[4 * a:, hc],
+                        rhs=v[a][:, hc].bitcast(FP8X4), rhs_scale=(v_sc_lo, v_sc_hi)[a][:, hc],
                         start=(a == 0), stop=(a == 1))
                 empty(("b", 4 * b + t, h), rows[:, hc], acc[:])
-            nc.vector.tensor_copy(out=picked[b][:, t, :], in_=rows[:].indirect(pos_t[2][:]))
+            nc.vector.tensor_tensor(out=picked[b][:, t, :], in0=rows[:].indirect(pos_t[2][:]), in1=low[b][:, t, :], op=ALU.mult)
 
         HALF = M // 2
         z_codes = {}
@@ -204,40 +211,38 @@ def tile_list_wine_pairing_menu_kernel(tc, tab_words, tab_scales, offs, pos1, po
         def combine(b, h):
             z_woven[b, h] = work.tile([P, PACK * HALF], BF16, name="z_woven", bufs=2, align_bytes=64)
             cols = slice(h * HALF, (h + 1) * HALF)
-            nc.vector.tensor_tensor(out=z_woven[b, h][:].rearrange("p (c i t) -> p c t i", i=4, t=PACK),
-                                    in0=low[b][:, :, cols].rearrange("p t (c i) -> p c t i", i=4),
-                                    in1=picked[b][:, :, cols].rearrange("p t (c i) -> p c t i", i=4), op=ALU.mult)
+            (nc.scalar.copy if (b, h) in ((1, 1),) else nc.vector.tensor_copy)(out=z_woven[b, h][:].rearrange("p (c i t) -> p c t i", i=4, t=PACK),
+                                  in_=picked[b][:, :, cols].rearrange("p t (c i) -> p c t i", i=4))
 
         def quantize_z(b, h):
-            z_codes[b, h] = held("z_codes%d_%d" % (b, h), [P, HALF], U32)
-            z_scales[b, h] = held("z_scales%d_%d" % (b, h), [P, HALF], U8)
-            nc.vector.quantize_mx(out=z_codes[b, h][:].bitcast(FP8X4), scales=z_scales[b, h][:], in_=z_woven[b, h][:])
+            if h == 0:
+                z_codes[b] = held("z_codes%d" % b, [P, M], U32)
+                z_scales[b] = held("z_scales%d" % b, [P, M], U8)
+            hc = slice(h * HALF, (h + 1) * HALF)
+            nc.vector.quantize_mx(out=z_codes[b][:, hc].bitcast(FP8X4), scales=z_scales[b][:, hc], in_=z_woven[b, h][:])
 
-        def second_stage(j, h):
-            acc = psum.tile([P, 2, HALF], F32, name="acc")
+        banks = {}
+
+        def second_stage(kind, j, a, h):
+            if (kind, j) not in banks:
+                banks[kind, j] = psum.tile([P, M], F32, name="acc")
             cols = slice(j * P, (j + 1) * P)
-            for a in range(2):
-                nc.tensor.matmul_mx(out=acc[:, 0, :], lhsT=codes[("w3", a)][:, cols].bitcast(FP8X4),
-                                    lhsT_scale=scales[("w3", a)][:, cols], rhs=z_codes[a, h][:].bitcast(FP8X4),
-                                    rhs_scale=z_scales[a, h][:], start=(a == 0), stop=(a == 1))
-            for a in range(2):
-                nc.tensor.matmul_mx(out=acc[:, 1, :], lhsT=w4[:, a, cols].bitcast(FP8X4),
-                                    lhsT_scale=w4_sc[4 * a:, cols], rhs=z_codes[a, h][:].bitcast(FP8X4),
-                                    rhs_scale=z_scales[a, h][:], start=(a == 0), stop=(a == 1))
-            gate = work.tile([P, HALF], F32, name="gate", bufs=8)
-            nc.scalar.activation(out=gate[:], in_=acc[:, 0, :], func=ACT.Sigmoid)
-            nc.vector.tensor_tensor(out=gate[:], in0=acc[:, 1, :], in1=gate[:], op=ALU.mult)
-            return gate
-
-        def finish(j, h, change, engine):
-            cols = slice(h * HALF, (h + 1) * HALF)
-            engine.tensor_tensor(out=change[:], in0=change[:], in1=house_t[:, j, cols], op=ALU.add)
-            nc.sync.dma_start(out=out[j * P:(j + 1) * P, cols], in_=change[:])
+            if kind == "e":
+                lhs, lhs_sc = codes[("w3", a)][:, cols], scales[("w3", a)][:, cols]
+            else:
+                lhs, lhs_sc = w4[:, a, cols], w4_sc[4 * a:, cols]
+            hc = slice(h * HALF, (h + 1) * HALF)
+            nc.tensor.matmul_mx(out=banks[kind, j][:, hc], lhsT=lhs.bitcast(FP8X4), lhsT_scale=lhs_sc,
+                                rhs=z_codes[a][:, hc].bitcast(FP8X4), rhs_scale=z_scales[a][:, hc],
+                                start=(a == 0), stop=(a == 1))
 
         gather_scales()
         gather_words(0)
+        load_rows(("w2", 0, 0))
         load_rows(("w2", 1, 0))
-        load_pos()
+        load_pos(0)
+        load_pos(1)
+        load_pos(2)
         load_rows(("w2", 0, 1))
         load_rows(("w2", 1, 1))
         load_w1(1)
@@ -246,8 +251,8 @@ def tile_list_wine_pairing_menu_kernel(tc, tab_words, tab_scales, offs, pos1, po
         order_w1_scales(0)
         order_w1(0)
         lower(0, 0, dish(0, 0))
-        weave_quantize(("w2", 0, 0), "sv")
-        weave_quantize(("w2", 1, 0), "vv")
+        weave_quantize(("w2", 0, 0), "v")
+        weave_quantize(("w2", 1, 0), "v")
         lower(0, 1, dish(0, 1))
         order_w1_scales(1)
         order_w1(1)
@@ -257,27 +262,41 @@ def tile_list_wine_pairing_menu_kernel(tc, tab_words, tab_scales, offs, pos1, po
             if i + 2 < 8:
                 nb, nt = divmod(i + 2, 4)
                 lower(nb, nt, dish(nb, nt))
-            if i in (1, 2):
-                weave_quantize(("w2", (1, 2).index(i), 1), "sv")
+            if i in (0, 1):
+                weave_quantize(("w2", (0, 1).index(i), 1), ("v", "v")[(0, 1).index(i)])
             if i == 3:
                 combine(0, 0)
                 combine(0, 1)
             if i == 4:
                 quantize_z(0, 0)
                 quantize_z(0, 1)
-            if i in ():
-                weave_quantize(("w3", ().index(i)), "ss")
-        for a in range(2):
-            weave_quantize(("w3", a), "ss")
+            if i in (6, 7):
+                weave_quantize(("w3", (6, 7).index(i)), "ss")
         combine(1, 0)
         combine(1, 1)
         quantize_z(1, 0)
         quantize_z(1, 1)
-        steps = [(j, h) for h in range(2) for j in range(4)]
+        for kind in "de":
+            for j in range(4):
+                second_stage(kind, j, 0, 0)
+
+        def finish(j, h, change):
+            hc = slice(h * HALF, (h + 1) * HALF)
+            nc.vector.tensor_tensor(out=change[:], in0=change[:], in1=house_t[:, j, hc], op=ALU.add)
+            nc.sync.dma_start(out=out[j * P:(j + 1) * P, hc], in_=change[:])
+
         last = None
-        for i, (j, h) in enumerate(steps):
-            change = second_stage(j, h)
-            if last is not None:
-                finish(*last)
-            last = (j, h, change, nc.vector)
+        for h in range(2):
+            for j in range(4):
+                for kind in "ed":
+                    for a in range(1 - h, 2):
+                        second_stage(kind, j, a, h)
+            hc = slice(h * HALF, (h + 1) * HALF)
+            for j in range(4):
+                gate = work.tile([P, HALF], F32, name="gate", bufs=8)
+                nc.scalar.activation(out=gate[:], in_=banks["e", j][:, hc], func=ACT.Sigmoid)
+                nc.vector.tensor_tensor(out=gate[:], in0=banks["d", j][:, hc], in1=gate[:], op=ALU.mult)
+                if last is not None:
+                    finish(*last)
+                last = (j, h, gate)
         finish(*last)

@@ -20,6 +20,14 @@ P = 128
 PACK = 4
 PASS = P * PACK
 BANK = 512
+QUAD = 32
+HALF = M // 2
+ROW_TILES = H // P
+LIVE = 24
+LIFT_ROWS = 100
+ROW_BUFS = 4
+DISH_AHEAD = 2
+POOL_PIECES = 6
 
 
 def tile_list_wine_pairing_menu_kernel(tc, tab_words, tab_scales, offs, pos1, pos2, pos3,
@@ -39,187 +47,170 @@ def tile_list_wine_pairing_menu_kernel(tc, tab_words, tab_scales, offs, pos1, po
 
         tab_sc = held("tab_sc", [P, T], U8)
         w1_sc_raw = held("w1_sc_raw", [P, 2, H], U8)
-        v_sc_hi = held("v_sc_hi", [P, S], U8)
-        v_sc_lo = held("v_sc_lo", [P, S], U8)
+        v_sc = [held("v_sc%d" % a, [P, S], U8) for a in range(2)]
         w4_sc = held("w4_sc", [P, N], U8)
         for q in range(4):
-            nc.vector.memset(tab_sc[32 * q: 32 * q + 24, :].bitcast(I32), 0)
+            nc.vector.memset(tab_sc[QUAD * q: QUAD * q + LIVE, :].bitcast(I32), 0)
         nc.vector.memset(w1_sc_raw[:].bitcast(I32), 0)
-        for plane in (v_sc_lo, v_sc_hi, w4_sc):
+        for plane in (v_sc[0], v_sc[1], w4_sc):
             nc.gpsimd.memset(plane[:].bitcast(I32), 0)
-        warm = held("warm", [P, 8], F32)
-        nc.vector.memset(warm[:, 0:4], 0.0)
-        nc.scalar.activation(out=warm[:, 4:8], in_=warm[:, 0:4], func=ACT.Sigmoid)
-
-        def load_scales(plane, scales):
-            for q in range(4):
-                nc.sync.dma_start(out=plane[32 * q: 32 * q + 8, :].bitcast(I32),
-                                  in_=scales[:, 4 * q: 4 * q + 4, :].bitcast(I32))
-
-        def load_w1_scales(queue):
-            for q in range(4):
-                queue.dma_start(out=w1_sc_raw[32 * q: 32 * q + 4, :, :].bitcast(I32),
-                                in_=w1_scales[:, 4 * q: 4 * q + 4, :].rearrange("a r c -> r a c").bitcast(I32))
-
-        def load_tab_scales():
-            for q in range(4):
-                nc.sync.dma_start(out=tab_sc[32 * q + 24: 32 * q + 32, :].bitcast(I32),
-                                  in_=tab_scales[:, 4 * q: 4 * q + 4, :].bitcast(I32))
 
         tab = [held("tab%d" % a, [P, T], I32) for a in range(2)]
         w1_raw = [held("w1_raw%d" % b, [P, 2, 2 * BANK], U8) for b in range(2)]
         w4 = held("w4", [P, 2, N], I32)
-        house_t = held("house_t", [P, 4, M], F32)
+        house_t = held("house_t", [P, N // P, M], F32)
         raw = {}
 
-        def load_tab(a):
-            nc.sync.dma_start(out=tab[a][:], in_=tab_words[a].rearrange("p t i -> p (t i)").bitcast(I32))
-
-        def load_rows(key):
-            if key[0] == "w2":
-                rows = w2[key[1] * PASS:(key[1] + 1) * PASS, key[2] * BANK:(key[2] + 1) * BANK]
-            else:
-                rows = w3[key[1] * PASS:(key[1] + 1) * PASS, :]
-            raw[key] = work.tile([P, PACK, BANK], F32, name="raw", bufs=4)
-            nc.sync.dma_start(out=raw[key][:], in_=rows.rearrange("(p j) c -> p j c", j=PACK))
+        def load_scales_of_both_passes(plane, first, scales):
+            for q in range(4):
+                nc.sync.dma_start(out=plane[QUAD * q + first: QUAD * q + first + 8, :].bitcast(I32),
+                                  in_=scales[:, 4 * q: 4 * q + 4, :].bitcast(I32))
 
         def load_w1(b):
             nc.sync.dma_start(out=w1_raw[b][:].bitcast(I32),
                               in_=w1_words[:, :, 2 * b * BANK: 2 * (b + 1) * BANK].rearrange("a p c -> p a c").bitcast(I32))
 
-        def load_pos(i):
-            nc.sync.dma_start(pos_t[i][:], (pos1, pos2, pos3)[i])
+        def load_rows(key, rows):
+            raw[key] = work.tile([P, PACK, BANK], F32, name="raw", bufs=4)
+            nc.sync.dma_start(out=raw[key][:], in_=rows.rearrange("(p j) c -> p j c", j=PACK))
 
-        def load_tail():
+        def load_w2(b):
             for a in range(2):
-                load_rows(("w3", a))
-            load_scales(w4_sc, w4_scales)
-            nc.sync.dma_start(out=w4[:], in_=w4_words.rearrange("a p c i -> p a (c i)").bitcast(I32))
-            nc.sync.dma_start(out=house_t[:], in_=house.rearrange("(j p) m -> p j m", p=P))
+                load_rows(("w2", a, b), w2[a * PASS:(a + 1) * PASS, b * BANK:(b + 1) * BANK])
 
         nc.sync.dma_start(offs_t[:], offs)
-        load_tab_scales()
-        load_tab(0)
-        load_tab(1)
+        load_scales_of_both_passes(tab_sc, LIVE, tab_scales)
+        for a in range(2):
+            nc.sync.dma_start(out=tab[a][:], in_=tab_words[a].rearrange("p t i -> p (t i)").bitcast(I32))
         load_w1(0)
-        load_w1_scales(nc.sync)
+        for q in range(4):
+            nc.sync.dma_start(out=w1_sc_raw[QUAD * q: QUAD * q + 4, :, :].bitcast(I32),
+                              in_=w1_scales[:, 4 * q: 4 * q + 4, :].rearrange("a r c -> r a c").bitcast(I32))
 
+        picked_sc = held("picked_sc", [P, S], U8)
+        nc.vector.tensor_copy(out=picked_sc[:], in_=tab_sc[:].indirect(offs_t[:]))
+        for a in range(2):
+            first = LIVE + 4 * a
+            nc.sync.dma_start(out=v_sc[a][0:LIFT_ROWS, :].bitcast(I32),
+                              in_=picked_sc[first:first + LIFT_ROWS, :].bitcast(I32))
         v = [held("v%d" % a, [P, S], U32) for a in range(2)]
-        v_sc = held("v_sc", [P, S], U8)
-        w1_sc = [held("w1_sc%d" % b, [P, 2, BANK], U8) for b in range(2)]
-        w1 = [held("w1_%d" % b, [P, 2, 2 * BANK], U8) for b in range(2)]
 
         def gather_words(a):
             nc.vector.tensor_copy(out=v[a][:], in_=tab[a][:].bitcast(U32).indirect(offs_t[:]))
 
-        def lift(dst, src, by=4):
-            nc.sync.dma_start(out=dst[0:100, :].bitcast(I32), in_=src[by:by + 100, :].bitcast(I32))
+        gather_words(0)
+        load_w2(0)
+        for i, pos in enumerate((pos1, pos2, pos3)):
+            nc.sync.dma_start(pos_t[i][:], pos)
+        load_w2(1)
+        load_w1(1)
+        for a in range(2):
+            load_rows(("w3", a), w3[a * PASS:(a + 1) * PASS, :])
+        load_scales_of_both_passes(w4_sc, 0, w4_scales)
+        nc.sync.dma_start(out=w4[:], in_=w4_words.rearrange("a p c i -> p a (c i)").bitcast(I32))
+        nc.sync.dma_start(out=house_t[:], in_=house.rearrange("(j p) m -> p j m", p=P))
+        gather_words(1)
 
-        def gather_scales():
-            nc.vector.tensor_copy(out=v_sc[:], in_=tab_sc[:].indirect(offs_t[:]))
-            lift(v_sc_lo, v_sc, 24)
-            lift(v_sc_hi, v_sc, 28)
+        w1 = [held("w1_%d" % b, [P, 2, 2 * BANK], U8) for b in range(2)]
+        w1_sc = [held("w1_sc%d" % b, [P, 2, BANK], U8) for b in range(2)]
 
-        def order_w1_scales(b):
+        def order_w1(b):
             nc.vector.tensor_copy(
                 out=w1_sc[b][:].rearrange("p a (t c i) -> p a c t i", t=PACK, i=16),
                 in_=w1_sc_raw[:, :, b * BANK:(b + 1) * BANK].rearrange("p a (c i t) -> p a c t i", t=PACK, i=16))
-
-        def order_w1(b):
             nc.vector.tensor_copy(
                 out=w1[b][:].bitcast(U16).rearrange("p a (t c i) -> p a c t i", t=PACK, i=8),
                 in_=w1_raw[b][:].bitcast(U16).rearrange("p a (c i t) -> p a c t i", t=PACK, i=8))
 
-        codes, scales, woven = {}, {}, {}
+        codes, scales = {}, {}
 
-        def pool_copy(out, in_):
-            nc.gpsimd.tensor_scalar(out=out, in0=in_, scalar1=1.0, scalar2=0.0, op0=ALU.mult, op1=ALU.add)
-
-        def weave(key, part, parts, engine):
-            if key not in woven:
-                woven[key] = work.tile([P, PACK * BANK], BF16, name="woven", bufs=3, align_bytes=64)
-            copy = {"v": nc.vector.tensor_copy, "s": nc.scalar.copy, "g": pool_copy}[engine]
-            cols = slice(part * P // parts, (part + 1) * P // parts)
+        def quantize_weight(key, copies):
+            woven = work.tile([P, PACK * BANK], BF16, name="woven", bufs=3, align_bytes=64)
             if key[0] == "w2":
-                copy(out=woven[key][:].rearrange("p (t m j) -> p m j t", t=PACK, j=PACK)[:, cols],
-                     in_=raw[key][:].rearrange("p j (m t) -> p m j t", t=PACK)[:, cols])
+                dst = woven[:].rearrange("p (t m j) -> p m j t", t=PACK, j=PACK)
             else:
-                copy(out=woven[key][:].rearrange("p (m i j) -> p m j i", i=PACK, j=PACK)[:, cols],
-                     in_=raw[key][:].rearrange("p j (m i) -> p m j i", i=PACK)[:, cols])
-
-        def quantize(key):
+                dst = woven[:].rearrange("p (m t j) -> p m j t", t=PACK, j=PACK)
+            src = raw[key][:].rearrange("p j (m t) -> p m j t", t=PACK)
+            share = P // len(copies)
+            for i, copy in enumerate(copies):
+                copy(out=dst[:, i * share:(i + 1) * share], in_=src[:, i * share:(i + 1) * share])
             name = "_".join(str(x) for x in key)
             codes[key] = held("codes_" + name, [P, BANK], U32)
             scales[key] = held("scales_" + name, [P, BANK], U8)
-            nc.vector.quantize_mx(out=codes[key][:].bitcast(FP8X4), scales=scales[key][:], in_=woven[key][:])
+            nc.vector.quantize_mx(out=codes[key][:].bitcast(FP8X4), scales=scales[key][:], in_=woven[:])
 
-        def weave_quantize(key, engines):
-            for part in range(len(engines)):
-                weave(key, part, len(engines), engines[part])
-            quantize(key)
+        on_vector = [nc.vector.tensor_copy]
+        on_scalar = [nc.scalar.copy] * 2
 
         low = [work.tile([P, PACK, M], F32, name="low%d" % b) for b in range(2)]
-        picked = [work.tile([P, PACK, M], F32, name="picked%d" % b) for b in range(2)]
+        z = [work.tile([P, PACK, M], F32, name="z%d" % b) for b in range(2)]
 
-        def empty(key, dst, acc):
-            if key in ():
-                nc.vector.tensor_copy(out=dst, in_=acc)
-            else:
-                nc.scalar.copy(out=dst, in_=acc)
-
-        def dish(b, t):
-            rows = work.tile([P, S], F32, name="dish_rows", bufs=4)
-            cols = slice(t * P, (t + 1) * P)
-            for h in range(2):
+        def first_stage(rows, passes, weight):
+            for h in range(S // BANK):
                 acc = psum.tile([P, BANK], F32, name="acc")
-                hc = slice(h * BANK, (h + 1) * BANK)
-                for a in (1, 0):
-                    nc.tensor.matmul_mx(
-                        out=acc[:], lhsT=w1[b][:, a, 2 * t * P: 2 * (t + 1) * P].bitcast(FP4X4),
-                        lhsT_scale=w1_sc[b][:, a, cols],
-                        rhs=v[a][:, hc].bitcast(FP8X4), rhs_scale=(v_sc_lo, v_sc_hi)[a][:, hc],
-                        start=(a == 1), stop=(a == 0))
-                empty(("d", 4 * b + t, h), rows[:, hc], acc[:])
+                profiles = slice(h * BANK, (h + 1) * BANK)
+                for a in passes:
+                    lhs, lhs_sc = weight(a)
+                    nc.tensor.matmul_mx(out=acc[:], lhsT=lhs, lhsT_scale=lhs_sc,
+                                        rhs=v[a][:, profiles].bitcast(FP8X4), rhs_scale=v_sc[a][:, profiles],
+                                        start=(a == passes[0]), stop=(a == passes[-1]))
+                nc.scalar.copy(out=rows[:, profiles], in_=acc[:])
+
+        def dish(i):
+            b, t = divmod(i, PACK)
+            rows = work.tile([P, S], F32, name="dish_rows", bufs=ROW_BUFS)
+            first_stage(rows, (1, 0), lambda a: (w1[b][:, a, 2 * t * P: 2 * (t + 1) * P].bitcast(FP4X4),
+                                                 w1_sc[b][:, a, t * P:(t + 1) * P]))
             nc.scalar.activation(out=low[b][:, t, :], in_=rows[:].indirect(pos_t[0][:]), func=ACT.Sigmoid)
             main = work.tile([P, M], F32, name="main", bufs=2)
             nc.vector.tensor_copy(out=main[:], in_=rows[:].indirect(pos_t[1][:]))
-            return main
-
-        def lower(b, t, main):
             nc.vector.tensor_tensor(out=low[b][:, t, :], in0=low[b][:, t, :], in1=main[:], op=ALU.min)
 
-        def bottle(b, t):
-            rows = work.tile([P, S], F32, name="bottle_rows", bufs=4)
-            cols = slice(t * P, (t + 1) * P)
-            for h in range(2):
-                acc = psum.tile([P, BANK], F32, name="acc")
-                hc = slice(h * BANK, (h + 1) * BANK)
-                for a in range(2):
-                    nc.tensor.matmul_mx(
-                        out=acc[:], lhsT=codes[("w2", a, b)][:, cols].bitcast(FP8X4),
-                        lhsT_scale=scales[("w2", a, b)][:, cols],
-                        rhs=v[a][:, hc].bitcast(FP8X4), rhs_scale=(v_sc_lo, v_sc_hi)[a][:, hc],
-                        start=(a == 0), stop=(a == 1))
-                empty(("b", 4 * b + t, h), rows[:, hc], acc[:])
-            nc.vector.tensor_tensor(out=picked[b][:, t, :], in0=rows[:].indirect(pos_t[2][:]), in1=low[b][:, t, :], op=ALU.mult)
+        def bottle(i):
+            b, t = divmod(i, PACK)
+            rows = work.tile([P, S], F32, name="bottle_rows", bufs=ROW_BUFS)
+            first_stage(rows, (0, 1), lambda a: (codes["w2", a, b][:, t * P:(t + 1) * P].bitcast(FP8X4),
+                                                 scales["w2", a, b][:, t * P:(t + 1) * P]))
+            nc.vector.tensor_tensor(out=z[b][:, t, :], in0=rows[:].indirect(pos_t[2][:]), in1=low[b][:, t, :], op=ALU.mult)
 
-        HALF = M // 2
-        z_codes = {}
-        z_scales = {}
+        z_codes = [held("z_codes%d" % b, [P, M], U32) for b in range(2)]
+        z_scales = [held("z_scales%d" % b, [P, M], U8) for b in range(2)]
         z_woven = {}
 
-        def combine(b, h):
+        def weave_z(b, h, copy):
             z_woven[b, h] = work.tile([P, PACK * HALF], BF16, name="z_woven", bufs=2, align_bytes=64)
-            cols = slice(h * HALF, (h + 1) * HALF)
-            (nc.scalar.copy if (b, h) in ((1, 1),) else nc.vector.tensor_copy)(out=z_woven[b, h][:].rearrange("p (c i t) -> p c t i", i=4, t=PACK),
-                                  in_=picked[b][:, :, cols].rearrange("p t (c i) -> p c t i", i=4))
+            copy(out=z_woven[b, h][:].rearrange("p (c i t) -> p c t i", i=4, t=PACK),
+                 in_=z[b][:, :, h * HALF:(h + 1) * HALF].rearrange("p t (c i) -> p c t i", i=4))
 
         def quantize_z(b, h):
-            if h == 0:
-                z_codes[b] = held("z_codes%d" % b, [P, M], U32)
-                z_scales[b] = held("z_scales%d" % b, [P, M], U8)
-            hc = slice(h * HALF, (h + 1) * HALF)
-            nc.vector.quantize_mx(out=z_codes[b][:, hc].bitcast(FP8X4), scales=z_scales[b][:, hc], in_=z_woven[b, h][:])
+            menus = slice(h * HALF, (h + 1) * HALF)
+            nc.vector.quantize_mx(out=z_codes[b][:, menus].bitcast(FP8X4), scales=z_scales[b][:, menus],
+                                  in_=z_woven[b, h][:])
+
+        order_w1(0)
+        dish(0)
+        for a in range(2):
+            quantize_weight(("w2", a, 0), on_vector)
+        dish(1)
+        order_w1(1)
+        for i in range(ROW_TILES):
+            bottle(i)
+            if i + DISH_AHEAD < ROW_TILES:
+                dish(i + DISH_AHEAD)
+            if i < 2:
+                quantize_weight(("w2", i, 1), (on_vector, on_scalar)[i])
+            if i == PACK - 1:
+                for h in range(2):
+                    weave_z(0, h, nc.vector.tensor_copy)
+            if i == PACK:
+                for h in range(2):
+                    quantize_z(0, h)
+            if i >= ROW_TILES - 2:
+                quantize_weight(("w3", i - (ROW_TILES - 2)), on_scalar)
+        weave_z(1, 0, nc.vector.tensor_copy)
+        weave_z(1, 1, nc.scalar.copy)
+        for h in range(2):
+            quantize_z(1, h)
 
         banks = {}
 
@@ -227,76 +218,37 @@ def tile_list_wine_pairing_menu_kernel(tc, tab_words, tab_scales, offs, pos1, po
             if (kind, j) not in banks:
                 banks[kind, j] = psum.tile([P, M], F32, name="acc")
             cols = slice(j * P, (j + 1) * P)
+            menus = slice(h * HALF, (h + 1) * HALF)
             if kind == "e":
-                lhs, lhs_sc = codes[("w3", a)][:, cols], scales[("w3", a)][:, cols]
+                lhs, lhs_sc = codes["w3", a][:, cols], scales["w3", a][:, cols]
             else:
                 lhs, lhs_sc = w4[:, a, cols], w4_sc[4 * a:, cols]
-            hc = slice(h * HALF, (h + 1) * HALF)
-            nc.tensor.matmul_mx(out=banks[kind, j][:, hc], lhsT=lhs.bitcast(FP8X4), lhsT_scale=lhs_sc,
-                                rhs=z_codes[a][:, hc].bitcast(FP8X4), rhs_scale=z_scales[a][:, hc],
+            nc.tensor.matmul_mx(out=banks[kind, j][:, menus], lhsT=lhs.bitcast(FP8X4), lhsT_scale=lhs_sc,
+                                rhs=z_codes[a][:, menus].bitcast(FP8X4), rhs_scale=z_scales[a][:, menus],
                                 start=(a == 0), stop=(a == 1))
 
-        gather_scales()
-        gather_words(0)
-        load_rows(("w2", 0, 0))
-        load_rows(("w2", 1, 0))
-        load_pos(0)
-        load_pos(1)
-        load_pos(2)
-        load_rows(("w2", 0, 1))
-        load_rows(("w2", 1, 1))
-        load_w1(1)
-        load_tail()
-        gather_words(1)
-        order_w1_scales(0)
-        order_w1(0)
-        lower(0, 0, dish(0, 0))
-        weave_quantize(("w2", 0, 0), "v")
-        weave_quantize(("w2", 1, 0), "v")
-        lower(0, 1, dish(0, 1))
-        order_w1_scales(1)
-        order_w1(1)
-        for i in range(8):
-            b, t = divmod(i, 4)
-            bottle(b, t)
-            if i + 2 < 8:
-                nb, nt = divmod(i + 2, 4)
-                lower(nb, nt, dish(nb, nt))
-            if i in (0, 1):
-                weave_quantize(("w2", (0, 1).index(i), 1), ("v", "v")[(0, 1).index(i)])
-            if i == 3:
-                combine(0, 0)
-                combine(0, 1)
-            if i == 4:
-                quantize_z(0, 0)
-                quantize_z(0, 1)
-            if i in (6, 7):
-                weave_quantize(("w3", (6, 7).index(i)), "ss")
-        combine(1, 0)
-        combine(1, 1)
-        quantize_z(1, 0)
-        quantize_z(1, 1)
-        for kind in "de":
-            for j in range(4):
-                second_stage(kind, j, 0, 0)
-
         def finish(j, h, change):
-            hc = slice(h * HALF, (h + 1) * HALF)
-            nc.vector.tensor_tensor(out=change[:], in0=change[:], in1=house_t[:, j, hc], op=ALU.add)
-            nc.sync.dma_start(out=out[j * P:(j + 1) * P, hc], in_=change[:])
+            menus = slice(h * HALF, (h + 1) * HALF)
+            piece = h * (N // P) + j
+            engine = nc.gpsimd if piece % 2 == 0 and piece < POOL_PIECES else nc.vector
+            engine.tensor_tensor(out=change[:], in0=change[:], in1=house_t[:, j, menus], op=ALU.add)
+            nc.sync.dma_start(out=out[j * P:(j + 1) * P, menus], in_=change[:])
 
+        for kind in "de":
+            for j in range(N // P):
+                second_stage(kind, j, 0, 0)
         last = None
         for h in range(2):
-            for j in range(4):
+            menus = slice(h * HALF, (h + 1) * HALF)
+            for j in range(N // P):
                 for kind in "ed":
                     for a in range(1 - h, 2):
                         second_stage(kind, j, a, h)
-            hc = slice(h * HALF, (h + 1) * HALF)
-            for j in range(4):
-                gate = work.tile([P, HALF], F32, name="gate", bufs=8)
-                nc.scalar.activation(out=gate[:], in_=banks["e", j][:, hc], func=ACT.Sigmoid)
-                nc.vector.tensor_tensor(out=gate[:], in0=banks["d", j][:, hc], in1=gate[:], op=ALU.mult)
+            for j in range(N // P):
+                change = work.tile([P, HALF], F32, name="change", bufs=8)
+                nc.scalar.activation(out=change[:], in_=banks["e", j][:, menus], func=ACT.Sigmoid)
+                nc.vector.tensor_tensor(out=change[:], in0=banks["d", j][:, menus], in1=change[:], op=ALU.mult)
                 if last is not None:
                     finish(*last)
-                last = (j, h, gate)
+                last = (j, h, change)
         finish(*last)

@@ -54,6 +54,9 @@ def tile_list_wine_pairing_menu_kernel(tc, tab_words, tab_scales, offs, pos1, po
         nc.vector.memset(w1_sc_raw[:].bitcast(I32), 0)
         for plane in (v_sc[0], v_sc[1], w4_sc):
             nc.gpsimd.memset(plane[:].bitcast(I32), 0)
+        warm = held("warm", [P, 8], F32)
+        nc.vector.memset(warm[:, 0:4], 0.0)
+        nc.scalar.activation(out=warm[:, 4:8], in_=warm[:, 0:4], func=ACT.Sigmoid)
 
         tab = [held("tab%d" % a, [P, T], I32) for a in range(2)]
         w1_raw = [held("w1_raw%d" % b, [P, 2, 2 * BANK], U8) for b in range(2)]

@@ -23,11 +23,13 @@ BANK = 512
 QUAD = 32
 HALF = M // 2
 ROW_TILES = H // P
-LIVE = 24
-LIFT_ROWS = 100
-ROW_BUFS = 4
-DISH_AHEAD = 2
-POOL_PIECES = 6
+RAW_BUFS = 4
+HEAD_TILES = 1
+ROW_BUFS = {"dish": 4, "bottle": 8}
+ZNAME = {"0": "z0", "1a": "z1a", "1b": "z1b"}
+ON_SCALAR = ()
+Q0, Q1 = 1, 3
+LIVE = 16
 
 
 def tile_list_wine_pairing_menu_kernel(tc, tab_words, tab_scales, offs, pos1, pos2, pos3,
@@ -46,174 +48,195 @@ def tile_list_wine_pairing_menu_kernel(tc, tab_words, tab_scales, offs, pos1, po
         pos_t = [keep.tile([P, M // 16], U16, name="pos_t%d" % i) for i in range(3)]
 
         tab_sc = held("tab_sc", [P, T], U8)
-        w1_sc_raw = held("w1_sc_raw", [P, 2, H], U8)
+        w1_sc = held("w1_sc", [P, 2, H], U8)
         v_sc = [held("v_sc%d" % a, [P, S], U8) for a in range(2)]
         w4_sc = held("w4_sc", [P, N], U8)
-        for q in range(4):
-            nc.vector.memset(tab_sc[QUAD * q: QUAD * q + LIVE, :].bitcast(I32), 0)
-        nc.vector.memset(w1_sc_raw[:].bitcast(I32), 0)
-        for plane in (v_sc[0], v_sc[1], w4_sc):
-            nc.gpsimd.memset(plane[:].bitcast(I32), 0)
+        nc.vector.memset(w1_sc[:].bitcast(I32), 0)
+        for first, count in ((0, LIVE), (QUAD, LIVE), (2 * QUAD, 2 * QUAD)):
+            nc.vector.memset(tab_sc[first: first + count, :].bitcast(I32), 0)
+        nc.gpsimd.memset(w4_sc[:].bitcast(I32), 0)
         warm = held("warm", [P, 8], F32)
         nc.vector.memset(warm[:, 0:4], 0.0)
         nc.scalar.activation(out=warm[:, 4:8], in_=warm[:, 0:4], func=ACT.Sigmoid)
 
-        tab = [held("tab%d" % a, [P, T], I32) for a in range(2)]
-        w1_raw = [held("w1_raw%d" % b, [P, 2, 2 * BANK], U8) for b in range(2)]
-        w4 = held("w4", [P, 2, N], I32)
-        house_t = held("house_t", [P, N // P, M], F32)
+        tab = [work.tile([P, T], I32, name="tab%d" % a, align_bytes=64) for a in range(2)]
+        w1 = [held("w1%d" % b, [P, 2, 2 * BANK], U8) for b in range(2)]
         raw = {}
 
-        def load_scales_of_both_passes(plane, first, scales):
-            for q in range(4):
-                nc.sync.dma_start(out=plane[QUAD * q + first: QUAD * q + first + 8, :].bitcast(I32),
-                                  in_=scales[:, 4 * q: 4 * q + 4, :].bitcast(I32))
-
         def load_w1(b):
-            nc.sync.dma_start(out=w1_raw[b][:].bitcast(I32),
+            nc.sync.dma_start(out=w1[b][:].bitcast(I32),
                               in_=w1_words[:, :, 2 * b * BANK: 2 * (b + 1) * BANK].rearrange("a p c -> p a c").bitcast(I32))
 
         def load_rows(key, rows):
-            raw[key] = work.tile([P, PACK, BANK], F32, name="raw", bufs=4)
+            raw[key] = work.tile([P, PACK, BANK], F32, name="raw", bufs=RAW_BUFS)
             nc.sync.dma_start(out=raw[key][:], in_=rows.rearrange("(p j) c -> p j c", j=PACK))
 
-        def load_w2(b):
-            for a in range(2):
-                load_rows(("w2", a, b), w2[a * PASS:(a + 1) * PASS, b * BANK:(b + 1) * BANK])
+        def load_w2(a, b):
+            load_rows(("w2", a, b), w2[a * PASS:(a + 1) * PASS, b * BANK:(b + 1) * BANK])
+
+        def load_tab(a):
+            nc.sync.dma_start(out=tab[a][:], in_=tab_words[a].rearrange("p t i -> p (t i)").bitcast(I32))
 
         nc.sync.dma_start(offs_t[:], offs)
-        load_scales_of_both_passes(tab_sc, LIVE, tab_scales)
-        for a in range(2):
-            nc.sync.dma_start(out=tab[a][:], in_=tab_words[a].rearrange("p t i -> p (t i)").bitcast(I32))
-        load_w1(0)
+        by_parity = tab_scales.rearrange("a (u e r) t -> e (a u) r t", e=2, r=4)
+        for e in range(2):
+            nc.sync.dma_start(out=tab_sc[QUAD * e + LIVE: QUAD * (e + 1), :].bitcast(I32), in_=by_parity[e].bitcast(I32))
+        load_tab(0)
         for q in range(4):
-            nc.sync.dma_start(out=w1_sc_raw[QUAD * q: QUAD * q + 4, :, :].bitcast(I32),
+            nc.sync.dma_start(out=w1_sc[QUAD * q: QUAD * q + 4, :, :].bitcast(I32),
                               in_=w1_scales[:, 4 * q: 4 * q + 4, :].rearrange("a r c -> r a c").bitcast(I32))
+        nc.sync.dma_start(pos_t[0][:], pos1)
+        load_tab(1)
+        load_w1(0)
 
         picked_sc = held("picked_sc", [P, S], U8)
         nc.vector.tensor_copy(out=picked_sc[:], in_=tab_sc[:].indirect(offs_t[:]))
         for a in range(2):
-            first = LIVE + 4 * a
-            nc.sync.dma_start(out=v_sc[a][0:LIFT_ROWS, :].bitcast(I32),
-                              in_=picked_sc[first:first + LIFT_ROWS, :].bitcast(I32))
-        v = [held("v%d" % a, [P, S], U32) for a in range(2)]
+            for u in range(2):
+                first = LIVE + 8 * a + 4 * u
+                nc.sync.dma_start(out=v_sc[a][64 * u:64 * (u + 1), :].bitcast(I32),
+                               in_=picked_sc[first:first + 64, :].bitcast(I32))
+        v = [[None, None], [None, None]]
 
-        def gather_words(a):
-            nc.vector.tensor_copy(out=v[a][:], in_=tab[a][:].bitcast(U32).indirect(offs_t[:]))
+        def gather_words(a, h):
+            v[a][h] = held("v%d_%d" % (a, h), [P, BANK], U32)
+            nc.vector.tensor_copy(out=v[a][h][:], in_=tab[a][:].bitcast(U32).indirect(offs_t[:, 32 * h:32 * (h + 1)]))
 
-        gather_words(0)
-        load_w2(0)
-        for i, pos in enumerate((pos1, pos2, pos3)):
-            nc.sync.dma_start(pos_t[i][:], pos)
-        load_w2(1)
+        load_w2(0, 0)
+        nc.sync.dma_start(pos_t[1][:], pos2)
+        load_w2(1, 0)
         load_w1(1)
+        nc.sync.dma_start(pos_t[2][:], pos3)
+        load_w2(0, 1)
+        load_w2(1, 1)
         for a in range(2):
             load_rows(("w3", a), w3[a * PASS:(a + 1) * PASS, :])
-        load_scales_of_both_passes(w4_sc, 0, w4_scales)
-        nc.sync.dma_start(out=w4[:], in_=w4_words.rearrange("a p c i -> p a (c i)").bitcast(I32))
-        nc.sync.dma_start(out=house_t[:], in_=house.rearrange("(j p) m -> p j m", p=P))
-        gather_words(1)
+        for q in range(4):
+            nc.sync.dma_start(out=w4_sc[QUAD * q: QUAD * q + 8, :].bitcast(I32),
+                              in_=w4_scales[:, 4 * q: 4 * q + 4, :].bitcast(I32))
 
-        w1 = [held("w1_%d" % b, [P, 2, 2 * BANK], U8) for b in range(2)]
-        w1_sc = [held("w1_sc%d" % b, [P, 2, BANK], U8) for b in range(2)]
+        codes, scales, woven = {}, {}, {}
 
-        def order_w1(b):
-            nc.vector.tensor_copy(
-                out=w1_sc[b][:].rearrange("p a (t c i) -> p a c t i", t=PACK, i=16),
-                in_=w1_sc_raw[:, :, b * BANK:(b + 1) * BANK].rearrange("p a (c i t) -> p a c t i", t=PACK, i=16))
-            nc.vector.tensor_copy(
-                out=w1[b][:].bitcast(U16).rearrange("p a (t c i) -> p a c t i", t=PACK, i=8),
-                in_=w1_raw[b][:].bitcast(U16).rearrange("p a (c i t) -> p a c t i", t=PACK, i=8))
-
-        codes, scales = {}, {}
-
-        def quantize_weight(key, copies):
-            woven = work.tile([P, PACK * BANK], BF16, name="woven", bufs=3, align_bytes=64)
-            if key[0] == "w2":
-                dst = woven[:].rearrange("p (t m j) -> p m j t", t=PACK, j=PACK)
+        def weave_weight(key, copies):
+            if key == ("w3", 1):
+                woven[key] = work.tile([P, PACK * BANK], BF16, name="bottle_rows", bufs=ROW_BUFS["bottle"], align_bytes=64)
             else:
-                dst = woven[:].rearrange("p (m t j) -> p m j t", t=PACK, j=PACK)
+                woven[key] = work.tile([P, PACK * BANK], BF16, name="woven", bufs=3, align_bytes=64)
+            if key[0] == "w2":
+                dst = woven[key][:].rearrange("p (t m j) -> p m j t", t=PACK, j=PACK)
+            else:
+                dst = woven[key][:].rearrange("p (m t j) -> p m j t", t=PACK, j=PACK)
             src = raw[key][:].rearrange("p j (m t) -> p m j t", t=PACK)
             share = P // len(copies)
             for i, copy in enumerate(copies):
                 copy(out=dst[:, i * share:(i + 1) * share], in_=src[:, i * share:(i + 1) * share])
+
+        def quantize_weight(key):
             name = "_".join(str(x) for x in key)
-            codes[key] = held("codes_" + name, [P, BANK], U32)
+            if key not in codes:
+                codes[key] = held("codes_" + name, [P, BANK], U32)[:]
             scales[key] = held("scales_" + name, [P, BANK], U8)
-            nc.vector.quantize_mx(out=codes[key][:].bitcast(FP8X4), scales=scales[key][:], in_=woven[:])
+            nc.vector.quantize_mx(out=codes[key].bitcast(FP8X4), scales=scales[key][:], in_=woven[key][:])
 
         on_vector = [nc.vector.tensor_copy]
         on_scalar = [nc.scalar.copy] * 2
 
-        low = [work.tile([P, PACK, M], F32, name="low%d" % b) for b in range(2)]
-        z = [work.tile([P, PACK, M], F32, name="z%d" % b) for b in range(2)]
+        rows = {}
 
-        def first_stage(rows, passes, weight):
-            for h in range(S // BANK):
-                acc = psum.tile([P, BANK], F32, name="acc")
-                profiles = slice(h * BANK, (h + 1) * BANK)
-                for a in passes:
-                    lhs, lhs_sc = weight(a)
-                    nc.tensor.matmul_mx(out=acc[:], lhsT=lhs, lhsT_scale=lhs_sc,
-                                        rhs=v[a][:, profiles].bitcast(FP8X4), rhs_scale=v_sc[a][:, profiles],
-                                        start=(a == passes[0]), stop=(a == passes[-1]))
-                nc.scalar.copy(out=rows[:, profiles], in_=acc[:])
+        def first_stage(kind, i, h):
+            b, t = divmod(i, PACK)
+            if (kind, i) not in rows:
+                rows[kind, i] = work.tile([P, S], F32, name=kind + "_rows", bufs=ROW_BUFS[kind], align_bytes=64)
+            acc = psum.tile([P, BANK], F32, name="acc")
+            profiles = slice(h * BANK, (h + 1) * BANK)
+            for a in (1, 0):
+                if kind == "dish":
+                    lhs, lhs_sc = w1[b][:, a, 2 * t * P: 2 * (t + 1) * P].bitcast(FP4X4), w1_sc[:, a, i * P:(i + 1) * P]
+                else:
+                    lhs, lhs_sc = codes["w2", a, b][:, t * P:(t + 1) * P].bitcast(FP8X4), scales["w2", a, b][:, t * P:(t + 1) * P]
+                nc.tensor.matmul_mx(out=acc[:], lhsT=lhs, lhsT_scale=lhs_sc,
+                                    rhs=v[a][h][:].bitcast(FP8X4), rhs_scale=v_sc[a][:, profiles],
+                                    start=(a == 1), stop=(a == 0))
+            nc.scalar.copy(out=rows[kind, i][:, profiles], in_=acc[:])
+
+        parts = {"0": (0, 0, M), "1a": (1, 0, HALF), "1b": (1, HALF, M)}
+        low = {}
+        for part in parts:
+            low[part] = work.tile([P, PACK, parts[part][2] - parts[part][1]], F32, name="low" + part, align_bytes=64)
+        z = {}
 
         def dish(i):
             b, t = divmod(i, PACK)
-            rows = work.tile([P, S], F32, name="dish_rows", bufs=ROW_BUFS)
-            first_stage(rows, (1, 0), lambda a: (w1[b][:, a, 2 * t * P: 2 * (t + 1) * P].bitcast(FP4X4),
-                                                 w1_sc[b][:, a, t * P:(t + 1) * P]))
-            nc.scalar.activation(out=low[b][:, t, :], in_=rows[:].indirect(pos_t[0][:]), func=ACT.Sigmoid)
+            if i >= HEAD_TILES:
+                first_stage("dish", i, 0)
+            first_stage("dish", i, 1)
+            starter = work.tile([P, M], F32, name="starter", bufs=ROW_TILES)
+            nc.scalar.activation(out=starter[:], in_=rows["dish", i][:].indirect(pos_t[0][:]), func=ACT.Sigmoid)
             main = work.tile([P, M], F32, name="main", bufs=2)
-            nc.vector.tensor_copy(out=main[:], in_=rows[:].indirect(pos_t[1][:]))
-            nc.vector.tensor_tensor(out=low[b][:, t, :], in0=low[b][:, t, :], in1=main[:], op=ALU.min)
+            nc.vector.tensor_copy(out=main[:], in_=rows["dish", i][:].indirect(pos_t[1][:]))
+            nc.vector.tensor_tensor(out=starter[:], in0=starter[:], in1=main[:], op=ALU.min)
+            for part in parts:
+                if parts[part][0] == b:
+                    nc.sync.dma_start(out=low[part][QUAD * t: QUAD * (t + 1), :, :], in_=starter[:, parts[part][1]:parts[part][2]])
+
+        def times_bottle(part, t):
+            b, lo, hi = parts[part]
+            if part not in z:
+                z[part] = work.tile([P, PACK, hi - lo], F32, name=ZNAME[part])
+            nc.vector.tensor_tensor(out=z[part][:, t, :],
+                                    in0=rows["bottle", PACK * b + t][:].indirect(pos_t[2][:, lo // 16: hi // 16]),
+                                    in1=low[part][:, t, :], op=ALU.mult)
 
         def bottle(i):
-            b, t = divmod(i, PACK)
-            rows = work.tile([P, S], F32, name="bottle_rows", bufs=ROW_BUFS)
-            first_stage(rows, (0, 1), lambda a: (codes["w2", a, b][:, t * P:(t + 1) * P].bitcast(FP8X4),
-                                                 scales["w2", a, b][:, t * P:(t + 1) * P]))
-            nc.vector.tensor_tensor(out=z[b][:, t, :], in0=rows[:].indirect(pos_t[2][:]), in1=low[b][:, t, :], op=ALU.mult)
+            for h in range(2):
+                first_stage("bottle", i, h)
+            times_bottle(("0", "1a")[i // PACK], i % PACK)
 
-        z_codes = [held("z_codes%d" % b, [P, M], U32) for b in range(2)]
-        z_scales = [held("z_scales%d" % b, [P, M], U8) for b in range(2)]
-        z_woven = {}
+        z_codes, z_scales, z_woven = {}, {}, {}
 
-        def weave_z(b, h, copy):
-            z_woven[b, h] = work.tile([P, PACK * HALF], BF16, name="z_woven", bufs=2, align_bytes=64)
-            copy(out=z_woven[b, h][:].rearrange("p (c i t) -> p c t i", i=4, t=PACK),
-                 in_=z[b][:, :, h * HALF:(h + 1) * HALF].rearrange("p t (c i) -> p c t i", i=4))
+        def weave_z(part, copy):
+            b, lo, hi = parts[part]
+            z_woven[part] = work.tile([P, PACK * (hi - lo)], BF16, name="z_woven" + part, align_bytes=64)
+            copy(out=z_woven[part][:].rearrange("p (c i t) -> p c t i", i=4, t=PACK),
+                 in_=z[part][:].rearrange("p t (c i) -> p c t i", i=4))
 
-        def quantize_z(b, h):
-            menus = slice(h * HALF, (h + 1) * HALF)
-            nc.vector.quantize_mx(out=z_codes[b][:, menus].bitcast(FP8X4), scales=z_scales[b][:, menus],
-                                  in_=z_woven[b, h][:])
+        def quantize_z(part):
+            b, lo, hi = parts[part]
+            if part not in z_codes:
+                z_codes[part] = held("z_codes" + part, [P, hi - lo], U32)[:]
+            z_scales[part] = held("z_scales" + part, [P, hi - lo], U8)
+            nc.vector.quantize_mx(out=z_codes[part].bitcast(FP8X4), scales=z_scales[part][:], in_=z_woven[part][:])
 
-        order_w1(0)
-        dish(0)
-        for a in range(2):
-            quantize_weight(("w2", a, 0), on_vector)
-        dish(1)
-        order_w1(1)
+        gather_words(0, 0)
+        gather_words(0, 1)
+        gather_words(1, 0)
+        for i in range(HEAD_TILES):
+            first_stage("dish", i, 0)
+        gather_words(1, 1)
+        w2_keys = [("w2", a, b) for b in range(2) for a in range(2)] + [("w3", 0)]
         for i in range(ROW_TILES):
+            if i < len(w2_keys):
+                weave_weight(w2_keys[i], on_scalar if i in ON_SCALAR else on_vector)
+            dish(i)
+            if i < len(w2_keys):
+                quantize_weight(w2_keys[i])
+
+        def after_dish(shape, dtype):
+            return work.tile(shape, dtype, name="dish_rows", bufs=ROW_BUFS["dish"], align_bytes=64)
+
+        w4 = after_dish([P, 2, N], I32)
+        nc.sync.dma_start(out=w4[:], in_=w4_words.rearrange("a p c i -> p a (c i)").bitcast(I32))
+        for i in range(PACK):
             bottle(i)
-            if i + DISH_AHEAD < ROW_TILES:
-                dish(i + DISH_AHEAD)
-            if i < 2:
-                quantize_weight(("w2", i, 1), (on_vector, on_scalar)[i])
-            if i == PACK - 1:
-                for h in range(2):
-                    weave_z(0, h, nc.vector.tensor_copy)
-            if i == PACK:
-                for h in range(2):
-                    quantize_z(0, h)
-            if i >= ROW_TILES - 2:
-                quantize_weight(("w3", i - (ROW_TILES - 2)), on_scalar)
-        weave_z(1, 0, nc.vector.tensor_copy)
-        weave_z(1, 1, nc.scalar.copy)
-        for h in range(2):
-            quantize_z(1, h)
+        house_t = work.tile([P, N // P, M], F32, name="low0", align_bytes=64)
+        nc.sync.dma_start(out=house_t[:], in_=house.rearrange("(j p) m -> p j m", p=P))
+        for i in range(PACK, ROW_TILES):
+            bottle(i)
+        weave_weight(("w3", 1), on_scalar)
+        weave_z("0", nc.scalar.copy)
+        late_codes = work.tile([P, 2 * BANK], U32, name="low1a", align_bytes=64)
+        z_codes["0"], codes["w3", 1] = late_codes[:, :BANK], late_codes[:, BANK:]
+        quantize_weight(("w3", 1))
 
         banks = {}
 
@@ -226,32 +249,44 @@ def tile_list_wine_pairing_menu_kernel(tc, tab_words, tab_scales, offs, pos1, po
                 lhs, lhs_sc = codes["w3", a][:, cols], scales["w3", a][:, cols]
             else:
                 lhs, lhs_sc = w4[:, a, cols], w4_sc[4 * a:, cols]
+            part, at = (("0", menus), (("1a", "1b")[h], slice(0, HALF)))[a]
             nc.tensor.matmul_mx(out=banks[kind, j][:, menus], lhsT=lhs.bitcast(FP8X4), lhsT_scale=lhs_sc,
-                                rhs=z_codes[a][:, menus].bitcast(FP8X4), rhs_scale=z_scales[a][:, menus],
+                                rhs=z_codes[part][:, at].bitcast(FP8X4), rhs_scale=z_scales[part][:, at],
                                 start=(a == 0), stop=(a == 1))
 
-        def finish(j, h, change):
+        def finish(j, h, change, engine):
             menus = slice(h * HALF, (h + 1) * HALF)
-            piece = h * (N // P) + j
-            engine = nc.gpsimd if piece % 2 == 0 and piece < POOL_PIECES else nc.vector
             engine.tensor_tensor(out=change[:], in0=change[:], in1=house_t[:, j, menus], op=ALU.add)
             nc.sync.dma_start(out=out[j * P:(j + 1) * P, menus], in_=change[:])
 
-        for kind in "de":
-            for j in range(N // P):
-                second_stage(kind, j, 0, 0)
-        last = None
-        for h in range(2):
+        def epilogue(h, engines):
             menus = slice(h * HALF, (h + 1) * HALF)
-            for j in range(N // P):
-                for kind in "ed":
-                    for a in range(1 - h, 2):
-                        second_stage(kind, j, a, h)
+            last = None
             for j in range(N // P):
                 change = work.tile([P, HALF], F32, name="change", bufs=8)
                 nc.scalar.activation(out=change[:], in_=banks["e", j][:, menus], func=ACT.Sigmoid)
                 nc.vector.tensor_tensor(out=change[:], in0=banks["d", j][:, menus], in1=change[:], op=ALU.mult)
                 if last is not None:
                     finish(*last)
-                last = (j, h, change)
-        finish(*last)
+                last = (j, h, change, engines[j])
+            finish(*last)
+
+        weave_z("1a", nc.scalar.copy)
+        for t in range(PACK):
+            times_bottle("1b", t)
+            if t == Q0:
+                quantize_z("0")
+            if t == Q1:
+                quantize_z("1a")
+        for a in range(2):
+            for j in range(N // P):
+                for kind in "ed":
+                    second_stage(kind, j, a, 0)
+        weave_z("1b", nc.vector.tensor_copy)
+        quantize_z("1b")
+        epilogue(0, [nc.gpsimd] * 4)
+        for j in range(N // P):
+            for kind in "ed":
+                for a in range(2):
+                    second_stage(kind, j, a, 1)
+        epilogue(1, [nc.vector] * 4)

@@ -29,7 +29,7 @@ ROW_BUFS = {"dish": 4, "bottle": 8}
 ZNAME = {"0": "z0", "1a": "z1a", "1b": "z1b"}
 ON_SCALAR = ()
 Q0, Q1 = 1, 3
-LIVE = 16
+LIVE = 96
 
 
 def tile_list_wine_pairing_menu_kernel(tc, tab_words, tab_scales, offs, pos1, pos2, pos3,
@@ -49,11 +49,11 @@ def tile_list_wine_pairing_menu_kernel(tc, tab_words, tab_scales, offs, pos1, po
 
         tab_sc = held("tab_sc", [P, T], U8)
         w1_sc = held("w1_sc", [P, 2, H], U8)
-        v_sc = [held("v_sc%d" % a, [P, S], U8) for a in range(2)]
+        v_sc = held("v_sc", [P, 2, S], U8)
         w4_sc = held("w4_sc", [P, N], U8)
         nc.vector.memset(w1_sc[:].bitcast(I32), 0)
-        for first, count in ((0, LIVE), (QUAD, LIVE), (2 * QUAD, 2 * QUAD)):
-            nc.vector.memset(tab_sc[first: first + count, :].bitcast(I32), 0)
+        nc.vector.memset(tab_sc[0:LIVE, :].bitcast(I32), 0)
+        nc.vector.memset(v_sc[:].bitcast(I32), 0)
         nc.gpsimd.memset(w4_sc[:].bitcast(I32), 0)
         warm = held("warm", [P, 8], F32)
         nc.vector.memset(warm[:, 0:4], 0.0)
@@ -78,24 +78,20 @@ def tile_list_wine_pairing_menu_kernel(tc, tab_words, tab_scales, offs, pos1, po
             nc.sync.dma_start(out=tab[a][:], in_=tab_words[a].rearrange("p t i -> p (t i)").bitcast(I32))
 
         nc.sync.dma_start(offs_t[:], offs)
-        by_parity = tab_scales.rearrange("a (u e r) t -> e (a u) r t", e=2, r=4)
-        for e in range(2):
-            nc.sync.dma_start(out=tab_sc[QUAD * e + LIVE: QUAD * (e + 1), :].bitcast(I32), in_=by_parity[e].bitcast(I32))
+        nc.sync.dma_start(out=tab_sc[LIVE:, :].bitcast(I32), in_=tab_scales.rearrange("a r t -> r a t").bitcast(I32))
         load_tab(0)
-        for q in range(4):
-            nc.sync.dma_start(out=w1_sc[QUAD * q: QUAD * q + 4, :, :].bitcast(I32),
-                              in_=w1_scales[:, 4 * q: 4 * q + 4, :].rearrange("a r c -> r a c").bitcast(I32))
+        for r in range(4):
+            nc.sync.dma_start(out=w1_sc[r:P:QUAD, :, :].bitcast(I32),
+                              in_=w1_scales[:, r:16:4, :].rearrange("a q c -> q a c").bitcast(I32))
         nc.sync.dma_start(pos_t[0][:], pos1)
         load_tab(1)
         load_w1(0)
 
         picked_sc = held("picked_sc", [P, S], U8)
         nc.vector.tensor_copy(out=picked_sc[:], in_=tab_sc[:].indirect(offs_t[:]))
-        for a in range(2):
-            for u in range(2):
-                first = LIVE + 8 * a + 4 * u
-                nc.sync.dma_start(out=v_sc[a][64 * u:64 * (u + 1), :].bitcast(I32),
-                               in_=picked_sc[first:first + 64, :].bitcast(I32))
+        for q in (0, 2, 1, 3):
+            nc.sync.dma_start(out=v_sc[QUAD * q: QUAD * q + 4, :, :].bitcast(I32),
+                              in_=picked_sc[LIVE + 8 * q: LIVE + 8 * (q + 1), :].bitcast(I32))
         v = [[None, None], [None, None]]
 
         def gather_words(a, h):
@@ -149,14 +145,14 @@ def tile_list_wine_pairing_menu_kernel(tc, tab_words, tab_scales, offs, pos1, po
                 rows[kind, i] = work.tile([P, S], F32, name=kind + "_rows", bufs=ROW_BUFS[kind], align_bytes=64)
             acc = psum.tile([P, BANK], F32, name="acc")
             profiles = slice(h * BANK, (h + 1) * BANK)
-            for a in (1, 0):
+            for a in range(2):
                 if kind == "dish":
                     lhs, lhs_sc = w1[b][:, a, 2 * t * P: 2 * (t + 1) * P].bitcast(FP4X4), w1_sc[:, a, i * P:(i + 1) * P]
                 else:
                     lhs, lhs_sc = codes["w2", a, b][:, t * P:(t + 1) * P].bitcast(FP8X4), scales["w2", a, b][:, t * P:(t + 1) * P]
                 nc.tensor.matmul_mx(out=acc[:], lhsT=lhs, lhsT_scale=lhs_sc,
-                                    rhs=v[a][h][:].bitcast(FP8X4), rhs_scale=v_sc[a][:, profiles],
-                                    start=(a == 1), stop=(a == 0))
+                                    rhs=v[a][h][:].bitcast(FP8X4), rhs_scale=v_sc[:, a, profiles],
+                                    start=(a == 0), stop=(a == 1))
             nc.scalar.copy(out=rows[kind, i][:, profiles], in_=acc[:])
 
         parts = {"0": (0, 0, M), "1a": (1, 0, HALF), "1b": (1, HALF, M)}

@@ -98,7 +98,10 @@ def tile_list_wine_pairing_menu_kernel(tc, tab_words, tab_scales, offs, pos1, po
             v[a][h] = held("v%d_%d" % (a, h), [P, BANK], U32)
             nc.vector.tensor_copy(out=v[a][h][:], in_=tab[a][:].bitcast(U32).indirect(offs_t[:, 32 * h:32 * (h + 1)]))
 
-        load_w2(0, 0)
+        first_w2 = []
+        for u in range(2):
+            first_w2.append(work.tile([P, PACK, HALF], F32, name="first_w2_%d" % u))
+            nc.sync.dma_start(out=first_w2[u][:], in_=w2[0:PASS, u * HALF:(u + 1) * HALF].rearrange("(p j) c -> p j c", j=PACK))
         nc.sync.dma_start(pos_t[1][:], pos2)
         load_w2(1, 0)
         load_w1(1)
@@ -122,6 +125,10 @@ def tile_list_wine_pairing_menu_kernel(tc, tab_words, tab_scales, offs, pos1, po
                 dst = woven[key][:].rearrange("p (t m j) -> p m j t", t=PACK, j=PACK)
             else:
                 dst = woven[key][:].rearrange("p (m t j) -> p m j t", t=PACK, j=PACK)
+            if key == ("w2", 0, 0):
+                for u in range(2):
+                    nc.vector.tensor_copy(out=dst[:, u * 64:(u + 1) * 64], in_=first_w2[u][:].rearrange("p j (m t) -> p m j t", t=PACK))
+                return
             src = raw[key][:].rearrange("p j (m t) -> p m j t", t=PACK)
             share = P // len(copies)
             for i, copy in enumerate(copies):

@@ -29,6 +29,8 @@ ROW_BUFS = {"dish": 4, "bottle": 8}
 ZNAME = {"0": "z0", "1a": "z1a", "1b": "z1b"}
 ON_SCALAR = ()
 Q0, Q1 = 1, 3
+EARLY_W3 = []
+LATE_W3 = [("w3", 0), ("w3", 1)]
 LIVE = 96
 
 
@@ -117,7 +119,7 @@ def tile_list_wine_pairing_menu_kernel(tc, tab_words, tab_scales, offs, pos1, po
         codes, scales, woven = {}, {}, {}
 
         def weave_weight(key, copies):
-            if key == ("w3", 1):
+            if key in LATE_W3:
                 woven[key] = work.tile([P, PACK * BANK], BF16, name="bottle_rows", bufs=ROW_BUFS["bottle"], align_bytes=64)
             else:
                 woven[key] = work.tile([P, PACK * BANK], BF16, name="woven", bufs=3, align_bytes=64)
@@ -185,7 +187,7 @@ def tile_list_wine_pairing_menu_kernel(tc, tab_words, tab_scales, offs, pos1, po
         def times_bottle(part, t):
             b, lo, hi = parts[part]
             if part not in z:
-                z[part] = work.tile([P, PACK, hi - lo], F32, name=ZNAME[part])
+                z[part] = work.tile([P, PACK, hi - lo], F32, name=ZNAME[part], align_bytes=64)
             nc.vector.tensor_tensor(out=z[part][:, t, :],
                                     in0=rows["bottle", PACK * b + t][:].indirect(pos_t[2][:, lo // 16: hi // 16]),
                                     in1=low[part][:, t, :], op=ALU.mult)
@@ -197,18 +199,17 @@ def tile_list_wine_pairing_menu_kernel(tc, tab_words, tab_scales, offs, pos1, po
 
         z_codes, z_scales, z_woven = {}, {}, {}
 
-        def weave_z(part, copy):
-            b, lo, hi = parts[part]
-            z_woven[part] = work.tile([P, PACK * (hi - lo)], BF16, name="z_woven" + part, align_bytes=64)
-            copy(out=z_woven[part][:].rearrange("p (c i t) -> p c t i", i=4, t=PACK),
-                 in_=z[part][:].rearrange("p t (c i) -> p c t i", i=4))
+        def weave_z(b, h, copy):
+            src = z["0"][:, :, h * HALF:(h + 1) * HALF] if b == 0 else z[("1a", "1b")[h]][:]
+            z_woven[b, h] = work.tile([P, PACK * HALF], BF16, name="z1a" if (b, h) == (0, 1) else "z_woven%d%d" % (b, h), align_bytes=64)
+            copy(out=z_woven[b, h][:].rearrange("p (c i t) -> p c t i", i=4, t=PACK),
+                 in_=src.rearrange("p t (c i) -> p c t i", i=4))
 
-        def quantize_z(part):
-            b, lo, hi = parts[part]
-            if part not in z_codes:
-                z_codes[part] = held("z_codes" + part, [P, hi - lo], U32)[:]
-            z_scales[part] = held("z_scales" + part, [P, hi - lo], U8)
-            nc.vector.quantize_mx(out=z_codes[part].bitcast(FP8X4), scales=z_scales[part][:], in_=z_woven[part][:])
+        def quantize_z(b, h):
+            if (b, h) not in z_codes:
+                z_codes[b, h] = held("z_codes%d%d" % (b, h), [P, HALF], U32)[:]
+            z_scales[b, h] = held("z_scales%d%d" % (b, h), [P, HALF], U8)
+            nc.vector.quantize_mx(out=z_codes[b, h].bitcast(FP8X4), scales=z_scales[b, h][:], in_=z_woven[b, h][:])
 
         gather_words(0, 0)
         gather_words(0, 1)
@@ -216,7 +217,7 @@ def tile_list_wine_pairing_menu_kernel(tc, tab_words, tab_scales, offs, pos1, po
         for i in range(HEAD_TILES):
             first_stage("dish", i, 0)
         gather_words(1, 1)
-        w2_keys = [("w2", a, b) for b in range(2) for a in range(2)] + [("w3", 0)]
+        w2_keys = [("w2", a, b) for b in range(2) for a in range(2)] + EARLY_W3
         for i in range(ROW_TILES):
             if i < len(w2_keys):
                 weave_weight(w2_keys[i], on_scalar if i in ON_SCALAR else on_vector)
@@ -235,11 +236,12 @@ def tile_list_wine_pairing_menu_kernel(tc, tab_words, tab_scales, offs, pos1, po
         nc.sync.dma_start(out=house_t[:], in_=house.rearrange("(j p) m -> p j m", p=P))
         for i in range(PACK, ROW_TILES):
             bottle(i)
-        weave_weight(("w3", 1), on_scalar)
-        weave_z("0", nc.scalar.copy)
-        late_codes = work.tile([P, 2 * BANK], U32, name="low1a", align_bytes=64)
-        z_codes["0"], codes["w3", 1] = late_codes[:, :BANK], late_codes[:, BANK:]
-        quantize_weight(("w3", 1))
+        for key in LATE_W3:
+            weave_weight(key, on_scalar)
+        late_codes = work.tile([P, 3 * BANK], U32, name="low1a", align_bytes=64)
+        z_codes[0, 0], z_codes[0, 1] = late_codes[:, :HALF], late_codes[:, HALF:BANK]
+        for key in LATE_W3:
+            codes[key] = late_codes[:, (1 + key[1]) * BANK:(2 + key[1]) * BANK]
 
         banks = {}
 
@@ -252,9 +254,8 @@ def tile_list_wine_pairing_menu_kernel(tc, tab_words, tab_scales, offs, pos1, po
                 lhs, lhs_sc = codes["w3", a][:, cols], scales["w3", a][:, cols]
             else:
                 lhs, lhs_sc = w4[:, a, cols], w4_sc[4 * a:, cols]
-            part, at = (("0", menus), (("1a", "1b")[h], slice(0, HALF)))[a]
             nc.tensor.matmul_mx(out=banks[kind, j][:, menus], lhsT=lhs.bitcast(FP8X4), lhsT_scale=lhs_sc,
-                                rhs=z_codes[part][:, at].bitcast(FP8X4), rhs_scale=z_scales[part][:, at],
+                                rhs=z_codes[a, h].bitcast(FP8X4), rhs_scale=z_scales[a, h][:],
                                 start=(a == 0), stop=(a == 1))
 
         def finish(j, h, change, engine):
@@ -274,19 +275,23 @@ def tile_list_wine_pairing_menu_kernel(tc, tab_words, tab_scales, offs, pos1, po
                 last = (j, h, change, engines[j])
             finish(*last)
 
-        weave_z("1a", nc.scalar.copy)
+        weave_z(0, 0, nc.vector.tensor_copy)
+        weave_z(1, 0, nc.scalar.copy)
+        weave_z(0, 1, nc.scalar.copy)
+        quantize_z(0, 0)
+        quantize_weight(("w3", 0))
         for t in range(PACK):
+            if t == PACK - 1:
+                quantize_weight(("w3", 1))
             times_bottle("1b", t)
-            if t == Q0:
-                quantize_z("0")
-            if t == Q1:
-                quantize_z("1a")
+        quantize_z(1, 0)
+        weave_z(1, 1, nc.vector.tensor_copy)
+        quantize_z(0, 1)
+        quantize_z(1, 1)
         for a in range(2):
             for j in range(N // P):
                 for kind in "ed":
                     second_stage(kind, j, a, 0)
-        weave_z("1b", nc.vector.tensor_copy)
-        quantize_z("1b")
         epilogue(0, [nc.gpsimd] * 4)
         for j in range(N // P):
             for kind in "ed":

@@ -31,6 +31,7 @@ ON_SCALAR = ()
 Q0, Q1 = 1, 3
 EARLY_W3 = []
 LATE_W3 = [("w3", 0), ("w3", 1)]
+FIRST = 256
 LIVE = 96
 
 
@@ -50,24 +51,31 @@ def tile_list_wine_pairing_menu_kernel(tc, tab_words, tab_scales, offs, pos1, po
         pos_t = [keep.tile([P, M // 16], U16, name="pos_t%d" % i) for i in range(3)]
 
         tab_sc = held("tab_sc", [P, T], U8)
-        w1_sc = held("w1_sc", [P, 2, H], U8)
+        w1_cols = [slice(0, FIRST), slice(FIRST, H)]
+        w1_sc = [held("w1_sc%d" % i, [P, 2, c.stop - c.start], U8) for i, c in enumerate(w1_cols)]
         v_sc = held("v_sc", [P, 2, S], U8)
         w4_sc = held("w4_sc", [P, N], U8)
-        nc.vector.memset(w1_sc[:].bitcast(I32), 0)
+        nc.vector.memset(w1_sc[0][:].bitcast(I32), 0)
         nc.vector.memset(tab_sc[0:LIVE, :].bitcast(I32), 0)
         nc.vector.memset(v_sc[:].bitcast(I32), 0)
+        nc.vector.memset(w1_sc[1][:].bitcast(I32), 0)
         nc.gpsimd.memset(w4_sc[:].bitcast(I32), 0)
         warm = held("warm", [P, 8], F32)
         nc.vector.memset(warm[:, 0:4], 0.0)
         nc.scalar.activation(out=warm[:, 4:8], in_=warm[:, 0:4], func=ACT.Sigmoid)
 
         tab = [work.tile([P, T], I32, name="tab%d" % a, align_bytes=64) for a in range(2)]
-        w1 = [held("w1%d" % b, [P, 2, 2 * BANK], U8) for b in range(2)]
+        w1 = [held("w1_%d" % i, [P, 2, 2 * (c.stop - c.start)], U8) for i, c in enumerate(w1_cols)]
         raw = {}
 
         def load_w1(b):
             nc.sync.dma_start(out=w1[b][:].bitcast(I32),
-                              in_=w1_words[:, :, 2 * b * BANK: 2 * (b + 1) * BANK].rearrange("a p c -> p a c").bitcast(I32))
+                              in_=w1_words[:, :, 2 * w1_cols[b].start: 2 * w1_cols[b].stop].rearrange("a p c -> p a c").bitcast(I32))
+
+        def load_w1_scales(b):
+            for r in range(4):
+                nc.sync.dma_start(out=w1_sc[b][r:P:QUAD, :, :].bitcast(I32),
+                                  in_=w1_scales[:, r:16:4, w1_cols[b]].rearrange("a q c -> q a c").bitcast(I32))
 
         def load_rows(key, rows):
             raw[key] = work.tile([P, PACK, BANK], F32, name="raw", bufs=RAW_BUFS)
@@ -82,9 +90,7 @@ def tile_list_wine_pairing_menu_kernel(tc, tab_words, tab_scales, offs, pos1, po
         nc.sync.dma_start(offs_t[:], offs)
         nc.sync.dma_start(out=tab_sc[LIVE:, :].bitcast(I32), in_=tab_scales.rearrange("a r t -> r a t").bitcast(I32))
         load_tab(0)
-        for r in range(4):
-            nc.sync.dma_start(out=w1_sc[r:P:QUAD, :, :].bitcast(I32),
-                              in_=w1_scales[:, r:16:4, :].rearrange("a q c -> q a c").bitcast(I32))
+        load_w1_scales(0)
         nc.sync.dma_start(pos_t[0][:], pos1)
         load_tab(1)
         load_w1(0)
@@ -105,8 +111,9 @@ def tile_list_wine_pairing_menu_kernel(tc, tab_words, tab_scales, offs, pos1, po
             first_w2.append(work.tile([P, PACK, HALF], F32, name="first_w2_%d" % u))
             nc.sync.dma_start(out=first_w2[u][:], in_=w2[0:PASS, u * HALF:(u + 1) * HALF].rearrange("(p j) c -> p j c", j=PACK))
         nc.sync.dma_start(pos_t[1][:], pos2)
-        load_w2(1, 0)
         load_w1(1)
+        load_w1_scales(1)
+        load_w2(1, 0)
         nc.sync.dma_start(pos_t[2][:], pos3)
         load_w2(0, 1)
         load_w2(1, 1)
@@ -154,9 +161,11 @@ def tile_list_wine_pairing_menu_kernel(tc, tab_words, tab_scales, offs, pos1, po
                 rows[kind, i] = work.tile([P, S], F32, name=kind + "_rows", bufs=ROW_BUFS[kind], align_bytes=64)
             acc = psum.tile([P, BANK], F32, name="acc")
             profiles = slice(h * BANK, (h + 1) * BANK)
+            late = int(i * P >= FIRST)
+            at = i * P - w1_cols[late].start
             for a in range(2):
                 if kind == "dish":
-                    lhs, lhs_sc = w1[b][:, a, 2 * t * P: 2 * (t + 1) * P].bitcast(FP4X4), w1_sc[:, a, i * P:(i + 1) * P]
+                    lhs, lhs_sc = w1[late][:, a, 2 * at: 2 * (at + P)].bitcast(FP4X4), w1_sc[late][:, a, at:at + P]
                 else:
                     lhs, lhs_sc = codes["w2", a, b][:, t * P:(t + 1) * P].bitcast(FP8X4), scales["w2", a, b][:, t * P:(t + 1) * P]
                 nc.tensor.matmul_mx(out=acc[:], lhsT=lhs, lhsT_scale=lhs_sc,

@@ -103,8 +103,8 @@ def tile_list_wine_pairing_menu_kernel(tc, tab_words, tab_scales, offs, pos1, po
         v = [[None, None], [None, None]]
 
         def gather_words(a, h):
-            v[a][h] = held("v%d_%d" % (a, h), [P, BANK], U32)
-            nc.vector.tensor_copy(out=v[a][h][:], in_=tab[a][:].bitcast(U32).indirect(offs_t[:, 32 * h:32 * (h + 1)]))
+            v[a][h] = held("v%d_%d" % (a, h), [P, BANK], U32)[:]
+            nc.vector.tensor_copy(out=v[a][h], in_=tab[a][:].bitcast(U32).indirect(offs_t[:, 32 * h:32 * (h + 1)]))
 
         first_w2 = []
         for u in range(2):
@@ -169,7 +169,7 @@ def tile_list_wine_pairing_menu_kernel(tc, tab_words, tab_scales, offs, pos1, po
                 else:
                     lhs, lhs_sc = codes["w2", a, b][:, t * P:(t + 1) * P].bitcast(FP8X4), scales["w2", a, b][:, t * P:(t + 1) * P]
                 nc.tensor.matmul_mx(out=acc[:], lhsT=lhs, lhsT_scale=lhs_sc,
-                                    rhs=v[a][h][:].bitcast(FP8X4), rhs_scale=v_sc[:, a, profiles],
+                                    rhs=v[a][h].bitcast(FP8X4), rhs_scale=v_sc[:, a, profiles],
                                     start=(a == 0), stop=(a == 1))
             nc.scalar.copy(out=rows[kind, i][:, profiles], in_=acc[:])
 
@@ -186,7 +186,7 @@ def tile_list_wine_pairing_menu_kernel(tc, tab_words, tab_scales, offs, pos1, po
             first_stage("dish", i, 1)
             starter = work.tile([P, M], F32, name="starter", bufs=ROW_TILES)
             nc.scalar.activation(out=starter[:], in_=rows["dish", i][:].indirect(pos_t[0][:]), func=ACT.Sigmoid)
-            main = work.tile([P, M], F32, name="main", bufs=2)
+            main = work.tile([P, M], F32, name="main", bufs=3)
             nc.vector.tensor_copy(out=main[:], in_=rows["dish", i][:].indirect(pos_t[1][:]))
             nc.vector.tensor_tensor(out=starter[:], in0=starter[:], in1=main[:], op=ALU.min)
             for part in parts:
@@ -220,8 +220,9 @@ def tile_list_wine_pairing_menu_kernel(tc, tab_words, tab_scales, offs, pos1, po
             z_scales[b, h] = held("z_scales%d%d" % (b, h), [P, HALF], U8)
             nc.vector.quantize_mx(out=z_codes[b, h].bitcast(FP8X4), scales=z_scales[b, h][:], in_=z_woven[b, h][:])
 
-        gather_words(0, 0)
-        gather_words(0, 1)
+        v0 = held("v0", [P, S], U32)
+        nc.vector.tensor_copy(out=v0[:], in_=tab[0][:].bitcast(U32).indirect(offs_t[:]))
+        v[0] = [v0[:, :BANK], v0[:, BANK:]]
         gather_words(1, 0)
         for i in range(HEAD_TILES):
             first_stage("dish", i, 0)
@@ -301,7 +302,7 @@ def tile_list_wine_pairing_menu_kernel(tc, tab_words, tab_scales, offs, pos1, po
             for j in range(N // P):
                 for kind in "ed":
                     second_stage(kind, j, a, 0)
-        epilogue(0, [nc.gpsimd] * 4)
+        epilogue(0, [nc.vector] * 4)
         for j in range(N // P):
             for kind in "ed":
                 for a in range(2):

@@ -33,6 +33,7 @@ EARLY_W3 = []
 LATE_W3 = [("w3", 0), ("w3", 1)]
 FIRST = 256
 LIVE = 96
+WARM_PASSES = 4
 
 
 def tile_list_wine_pairing_menu_kernel(tc, tab_words, tab_scales, offs, pos1, pos2, pos3,
@@ -220,9 +221,13 @@ def tile_list_wine_pairing_menu_kernel(tc, tab_words, tab_scales, offs, pos1, po
             z_scales[b, h] = held("z_scales%d%d" % (b, h), [P, HALF], U8)
             nc.vector.quantize_mx(out=z_codes[b, h].bitcast(FP8X4), scales=z_scales[b, h][:], in_=z_woven[b, h][:])
 
-        v0 = held("v0", [P, S], U32)
-        nc.vector.tensor_copy(out=v0[:], in_=tab[0][:].bitcast(U32).indirect(offs_t[:]))
-        v[0] = [v0[:, :BANK], v0[:, BANK:]]
+        gather_words(0, 0)
+        idle = psum.tile([P, BANK], F32, name="acc")
+        for n in range(WARM_PASSES):
+            nc.tensor.matmul_mx(out=idle[:], lhsT=v[0][0][:, :P].bitcast(FP8X4), lhsT_scale=picked_sc[:, :P],
+                                rhs=v[0][0].bitcast(FP8X4), rhs_scale=picked_sc[:, :BANK],
+                                start=(n == 0), stop=(n == WARM_PASSES - 1))
+        gather_words(0, 1)
         gather_words(1, 0)
         for i in range(HEAD_TILES):
             first_stage("dish", i, 0)

@@ -24,7 +24,7 @@ QUAD = 32
 HALF = M // 2
 ROW_TILES = H // P
 RAW_BUFS = 4
-HEAD_TILES = 1
+HEAD_TILES = 2
 ROW_BUFS = {"dish": 4, "bottle": 8}
 ZNAME = {"0": "z0", "1a": "z1a", "1b": "z1b"}
 ON_SCALAR = ()
@@ -33,6 +33,7 @@ EARLY_W3 = []
 LATE_W3 = [("w3", 0), ("w3", 1)]
 FIRST = 256
 LIVE = 96
+FIRST_CUTS = [(0, 256), (256, 384), (384, 512)]
 WARM_PASSES = 4
 
 
@@ -108,9 +109,9 @@ def tile_list_wine_pairing_menu_kernel(tc, tab_words, tab_scales, offs, pos1, po
             nc.vector.tensor_copy(out=v[a][h], in_=tab[a][:].bitcast(U32).indirect(offs_t[:, 32 * h:32 * (h + 1)]))
 
         first_w2 = []
-        for u in range(2):
-            first_w2.append(work.tile([P, PACK, HALF], F32, name="first_w2_%d" % u))
-            nc.sync.dma_start(out=first_w2[u][:], in_=w2[0:PASS, u * HALF:(u + 1) * HALF].rearrange("(p j) c -> p j c", j=PACK))
+        for u, (lo, hi) in enumerate(FIRST_CUTS):
+            first_w2.append(work.tile([P, PACK, hi - lo], F32, name="first_w2_%d" % u))
+            nc.sync.dma_start(out=first_w2[u][:], in_=w2[0:PASS, lo:hi].rearrange("(p j) c -> p j c", j=PACK))
         nc.sync.dma_start(pos_t[1][:], pos2)
         load_w1(1)
         load_w1_scales(1)
@@ -136,8 +137,8 @@ def tile_list_wine_pairing_menu_kernel(tc, tab_words, tab_scales, offs, pos1, po
             else:
                 dst = woven[key][:].rearrange("p (m t j) -> p m j t", t=PACK, j=PACK)
             if key == ("w2", 0, 0):
-                for u in range(2):
-                    nc.vector.tensor_copy(out=dst[:, u * 64:(u + 1) * 64], in_=first_w2[u][:].rearrange("p j (m t) -> p m j t", t=PACK))
+                for u, (lo, hi) in enumerate(FIRST_CUTS):
+                    nc.vector.tensor_copy(out=dst[:, lo // PACK:hi // PACK], in_=first_w2[u][:].rearrange("p j (m t) -> p m j t", t=PACK))
                 return
             src = raw[key][:].rearrange("p j (m t) -> p m j t", t=PACK)
             share = P // len(copies)

@@ -33,7 +33,8 @@ EARLY_W3 = []
 LATE_W3 = [("w3", 0), ("w3", 1)]
 FIRST = 256
 LIVE = 96
-FIRST_CUTS = [(0, 256), (256, 384), (384, 512)]
+WOVEN = 2 * PACK * HALF
+FIRST_CUTS = [(0, 512)]
 WARM_PASSES = 4
 
 
@@ -44,6 +45,7 @@ def tile_list_wine_pairing_menu_kernel(tc, tab_words, tab_scales, offs, pos1, po
     with ExitStack() as ctx:
         keep = ctx.enter_context(tc.tile_pool(name="keep", bufs=1))
         work = ctx.enter_context(tc.tile_pool(name="work", bufs=1))
+        late = ctx.enter_context(tc.tile_pool(name="late", bufs=1))
         psum = ctx.enter_context(tc.psum_pool(name="psum", bufs=8))
 
         def held(name, shape, dtype):
@@ -163,11 +165,11 @@ def tile_list_wine_pairing_menu_kernel(tc, tab_words, tab_scales, offs, pos1, po
                 rows[kind, i] = work.tile([P, S], F32, name=kind + "_rows", bufs=ROW_BUFS[kind], align_bytes=64)
             acc = psum.tile([P, BANK], F32, name="acc")
             profiles = slice(h * BANK, (h + 1) * BANK)
-            late = int(i * P >= FIRST)
-            at = i * P - w1_cols[late].start
+            piece = int(i * P >= FIRST)
+            at = i * P - w1_cols[piece].start
             for a in range(2):
                 if kind == "dish":
-                    lhs, lhs_sc = w1[late][:, a, 2 * at: 2 * (at + P)].bitcast(FP4X4), w1_sc[late][:, a, at:at + P]
+                    lhs, lhs_sc = w1[piece][:, a, 2 * at: 2 * (at + P)].bitcast(FP4X4), w1_sc[piece][:, a, at:at + P]
                 else:
                     lhs, lhs_sc = codes["w2", a, b][:, t * P:(t + 1) * P].bitcast(FP8X4), scales["w2", a, b][:, t * P:(t + 1) * P]
                 nc.tensor.matmul_mx(out=acc[:], lhsT=lhs, lhsT_scale=lhs_sc,
@@ -178,7 +180,10 @@ def tile_list_wine_pairing_menu_kernel(tc, tab_words, tab_scales, offs, pos1, po
         parts = {"0": (0, 0, M), "1a": (1, 0, HALF), "1b": (1, HALF, M)}
         low = {}
         for part in parts:
-            low[part] = work.tile([P, PACK, parts[part][2] - parts[part][1]], F32, name="low" + part, align_bytes=64)
+            if part == "1a":
+                low[part] = late.tile([P, PACK, HALF], F32, name="low1a", align_bytes=64, offset=WOVEN - 64)
+            else:
+                low[part] = work.tile([P, PACK, parts[part][2] - parts[part][1]], F32, name="low" + part, align_bytes=64)
         z = {}
 
         def dish(i):
@@ -190,6 +195,13 @@ def tile_list_wine_pairing_menu_kernel(tc, tab_words, tab_scales, offs, pos1, po
             nc.scalar.activation(out=starter[:], in_=rows["dish", i][:].indirect(pos_t[0][:]), func=ACT.Sigmoid)
             main = work.tile([P, M], F32, name="main", bufs=3)
             nc.vector.tensor_copy(out=main[:], in_=rows["dish", i][:].indirect(pos_t[1][:]))
+            picks[i] = (starter, main)
+
+        picks = {}
+
+        def least(i):
+            b, t = divmod(i, PACK)
+            starter, main = picks[i]
             nc.vector.tensor_tensor(out=starter[:], in0=starter[:], in1=main[:], op=ALU.min)
             for part in parts:
                 if parts[part][0] == b:
@@ -212,7 +224,10 @@ def tile_list_wine_pairing_menu_kernel(tc, tab_words, tab_scales, offs, pos1, po
 
         def weave_z(b, h, copy):
             src = z["0"][:, :, h * HALF:(h + 1) * HALF] if b == 0 else z[("1a", "1b")[h]][:]
-            z_woven[b, h] = work.tile([P, PACK * HALF], BF16, name="z1a" if (b, h) == (0, 1) else "z_woven%d%d" % (b, h), align_bytes=64)
+            if b == 0:
+                z_woven[b, h] = late.tile([P, PACK * HALF], BF16, name="z_woven0%d" % h, align_bytes=64, offset=h * WOVEN)
+            else:
+                z_woven[b, h] = work.tile([P, PACK * HALF], BF16, name="z_woven%d%d" % (b, h), align_bytes=64)
             copy(out=z_woven[b, h][:].rearrange("p (c i t) -> p c t i", i=4, t=PACK),
                  in_=src.rearrange("p t (c i) -> p c t i", i=4))
 
@@ -238,8 +253,11 @@ def tile_list_wine_pairing_menu_kernel(tc, tab_words, tab_scales, offs, pos1, po
             if i < len(w2_keys):
                 weave_weight(w2_keys[i], on_scalar if i in ON_SCALAR else on_vector)
             dish(i)
+            if i > 0:
+                least(i - 1)
             if i < len(w2_keys):
                 quantize_weight(w2_keys[i])
+        least(ROW_TILES - 1)
 
         def after_dish(shape, dtype):
             return work.tile(shape, dtype, name="dish_rows", bufs=ROW_BUFS["dish"], align_bytes=64)
@@ -254,7 +272,7 @@ def tile_list_wine_pairing_menu_kernel(tc, tab_words, tab_scales, offs, pos1, po
             bottle(i)
         for key in LATE_W3:
             weave_weight(key, on_scalar)
-        late_codes = work.tile([P, 3 * BANK], U32, name="low1a", align_bytes=64)
+        late_codes = late.tile([P, 3 * BANK], U32, name="late_codes", align_bytes=64, offset=2 * WOVEN)
         z_codes[0, 0], z_codes[0, 1] = late_codes[:, :HALF], late_codes[:, HALF:BANK]
         for key in LATE_W3:
             codes[key] = late_codes[:, (1 + key[1]) * BANK:(2 + key[1]) * BANK]
@@ -294,8 +312,8 @@ def tile_list_wine_pairing_menu_kernel(tc, tab_words, tab_scales, offs, pos1, po
         weave_z(0, 0, nc.vector.tensor_copy)
         weave_z(1, 0, nc.scalar.copy)
         weave_z(0, 1, nc.scalar.copy)
-        quantize_z(0, 0)
         quantize_weight(("w3", 0))
+        quantize_z(0, 0)
         for t in range(PACK):
             if t == PACK - 1:
                 quantize_weight(("w3", 1))

@@ -61,12 +61,14 @@ def tile_list_wine_pairing_menu_kernel(tc, tab_words, tab_scales, offs, pos1, po
         w4_sc = held("w4_sc", [P, N], U8)
         nc.vector.memset(w1_sc[0][:].bitcast(I32), 0)
         nc.vector.memset(tab_sc[0:LIVE, :].bitcast(I32), 0)
-        nc.vector.memset(v_sc[:].bitcast(I32), 0)
-        nc.vector.memset(w1_sc[1][:].bitcast(I32), 0)
-        nc.gpsimd.memset(w4_sc[:].bitcast(I32), 0)
-        warm = held("warm", [P, 8], F32)
-        nc.vector.memset(warm[:, 0:4], 0.0)
-        nc.scalar.activation(out=warm[:, 4:8], in_=warm[:, 0:4], func=ACT.Sigmoid)
+        zeros = held("zeros", [P, P], I32)
+        nc.vector.memset(zeros[:], 0)
+        warm = held("warm", [P, 4], F32)
+        nc.scalar.activation(out=warm[:], in_=zeros[:, 0:4].bitcast(F32), func=ACT.Sigmoid)
+        for plane in (v_sc[:].rearrange("p a s -> p (a s)"), w1_sc[1][:].rearrange("p a s -> p (a s)"), w4_sc[:]):
+            words = plane.bitcast(U32)
+            for at in range(0, words.shape[1], P):
+                nc.scalar.copy(out=words[:, at:at + P], in_=zeros[:].bitcast(U32))
 
         tab = [work.tile([P, T], I32, name="tab%d" % a, align_bytes=64) for a in range(2)]
         w1 = [held("w1_%d" % i, [P, 2, 2 * (c.stop - c.start)], U8) for i, c in enumerate(w1_cols)]

@@ -195,7 +195,10 @@ def tile_list_wine_pairing_menu_kernel(tc, tab_words, tab_scales, offs, pos1, po
             first_stage("dish", i, 1)
             starter = work.tile([P, M], F32, name="starter", bufs=ROW_TILES)
             nc.scalar.activation(out=starter[:], in_=rows["dish", i][:].indirect(pos_t[0][:]), func=ACT.Sigmoid)
-            main = work.tile([P, M], F32, name="main", bufs=3)
+            if i == ROW_TILES - 1:
+                main = late.tile([P, M], F32, name="last_main", align_bytes=64, offset=6 * WOVEN)
+            else:
+                main = work.tile([P, M], F32, name="main", bufs=3)
             nc.vector.tensor_copy(out=main[:], in_=rows["dish", i][:].indirect(pos_t[1][:]))
             picks[i] = (starter, main)
 
@@ -261,10 +264,7 @@ def tile_list_wine_pairing_menu_kernel(tc, tab_words, tab_scales, offs, pos1, po
                 quantize_weight(w2_keys[i])
         least(ROW_TILES - 1)
 
-        def after_dish(shape, dtype):
-            return work.tile(shape, dtype, name="dish_rows", bufs=ROW_BUFS["dish"], align_bytes=64)
-
-        w4 = after_dish([P, 2, N], I32)
+        w4 = late.tile([P, 2, N], I32, name="w4", align_bytes=64, offset=6 * WOVEN)
         nc.sync.dma_start(out=w4[:], in_=w4_words.rearrange("a p c i -> p a (c i)").bitcast(I32))
         for i in range(PACK):
             bottle(i)

from contextlib import ExitStack

import concourse.mybir as mybir

K, H, N, T, S, M = 1024, 1024, 512, 2048, 1024, 512
FLOPS = 2 * (2 * K * H * S + 2 * H * N * M)

F32 = mybir.dt.float32
BF16 = mybir.dt.bfloat16
I32 = mybir.dt.int32
U32 = mybir.dt.uint32
U16 = mybir.dt.uint16
U8 = mybir.dt.uint8
FP8X4 = mybir.dt.float8_e4m3fn_x4
FP4X4 = mybir.dt.float4_e2m1fn_x4
ALU = mybir.AluOpType
ACT = mybir.ActivationFunctionType

P = 128
PACK = 4
PASS = P * PACK
BANK = 512
QUAD = 32
HALF = M // 2
ROW_TILES = H // P
RAW_BUFS = 4
HEAD_TILES = 2
ROW_BUFS = {"dish": 4, "bottle": 8}
ZNAME = {"0": "z0", "1a": "z1a", "1b": "z1b"}
ON_SCALAR = ()
Q0, Q1 = 1, 3
EARLY_W3 = []
LATE_W3 = [("w3", 0), ("w3", 1)]
FIRST = 256
LIVE = 96
WOVEN = 2 * PACK * HALF
FIRST_CUTS = [(0, 512)]
WARM_PASSES = 4


def tile_list_wine_pairing_menu_kernel(tc, tab_words, tab_scales, offs, pos1, pos2, pos3,
                                                 w1_words, w1_scales, w2, w3, w4_words, w4_scales,
                                                 house, out):
    nc = tc.nc
    with ExitStack() as ctx:
        keep = ctx.enter_context(tc.tile_pool(name="keep", bufs=1))
        work = ctx.enter_context(tc.tile_pool(name="work", bufs=1))
        late = ctx.enter_context(tc.tile_pool(name="late", bufs=1))
        psum = ctx.enter_context(tc.psum_pool(name="psum", bufs=8))

        def held(name, shape, dtype):
            return keep.tile(shape, dtype, name=name, align_bytes=64)

        offs_t = keep.tile([P, S // 16], U16, name="offs_t")
        pos_t = [keep.tile([P, M // 16], U16, name="pos_t%d" % i) for i in range(3)]

        tab_sc = held("tab_sc", [P, T], U8)
        w1_cols = [slice(0, FIRST), slice(FIRST, H)]
        w1_sc = [held("w1_sc%d" % i, [P, 2, c.stop - c.start], U8) for i, c in enumerate(w1_cols)]
        v_sc = held("v_sc", [P, 2, S], U8)
        w4_sc = held("w4_sc", [P, N], U8)
        nc.vector.memset(w1_sc[0][:].bitcast(I32), 0)
        nc.vector.memset(tab_sc[0:LIVE, :].bitcast(I32), 0)
        zeros = held("zeros", [P, P], I32)
        nc.vector.memset(zeros[:], 0)
        warm = held("warm", [P, 4], F32)
        nc.scalar.activation(out=warm[:], in_=zeros[:, 0:4].bitcast(F32), func=ACT.Sigmoid)
        for plane in (v_sc[:].rearrange("p a s -> p (a s)"), w1_sc[1][:].rearrange("p a s -> p (a s)"), w4_sc[:]):
            words = plane.bitcast(U32)
            for at in range(0, words.shape[1], P):
                nc.scalar.copy(out=words[:, at:at + P], in_=zeros[:].bitcast(U32))

        tab = [work.tile([P, T], I32, name="tab%d" % a, align_bytes=64) for a in range(2)]
        w1 = [held("w1_%d" % i, [P, 2, 2 * (c.stop - c.start)], U8) for i, c in enumerate(w1_cols)]
        raw = {}

        def load_w1(b):
            nc.sync.dma_start(out=w1[b][:].bitcast(I32),
                              in_=w1_words[:, :, 2 * w1_cols[b].start: 2 * w1_cols[b].stop].rearrange("a p c -> p a c").bitcast(I32))

        def load_w1_scales(b):
            for r in range(4):
                nc.sync.dma_start(out=w1_sc[b][r:P:QUAD, :, :].bitcast(I32),
                                  in_=w1_scales[:, r:16:4, w1_cols[b]].rearrange("a q c -> q a c").bitcast(I32))

        def load_rows(key, rows):
            raw[key] = work.tile([P, PACK, BANK], F32, name="raw", bufs=RAW_BUFS)
            nc.sync.dma_start(out=raw[key][:], in_=rows.rearrange("(p j) c -> p j c", j=PACK))

        def load_w2(a, b):
            load_rows(("w2", a, b), w2[a * PASS:(a + 1) * PASS, b * BANK:(b + 1) * BANK])

        def load_tab(a):
            nc.sync.dma_start(out=tab[a][:], in_=tab_words[a].rearrange("p t i -> p (t i)").bitcast(I32))

        nc.sync.dma_start(offs_t[:], offs)
        nc.sync.dma_start(out=tab_sc[LIVE:, :].bitcast(I32), in_=tab_scales.rearrange("a r t -> r a t").bitcast(I32))
        load_tab(0)
        load_w1_scales(0)
        nc.sync.dma_start(pos_t[0][:], pos1)
        load_tab(1)
        load_w1(0)

        picked_sc = held("picked_sc", [P, S], U8)
        nc.vector.tensor_copy(out=picked_sc[:], in_=tab_sc[:].indirect(offs_t[:]))
        for q in (0, 2, 1, 3):
            nc.sync.dma_start(out=v_sc[QUAD * q: QUAD * q + 4, :, :].bitcast(I32),
                              in_=picked_sc[LIVE + 8 * q: LIVE + 8 * (q + 1), :].bitcast(I32))
        v = [[None, None], [None, None]]

        def gather_words(a, h):
            v[a][h] = held("v%d_%d" % (a, h), [P, BANK], U32)[:]
            nc.vector.tensor_copy(out=v[a][h], in_=tab[a][:].bitcast(U32).indirect(offs_t[:, 32 * h:32 * (h + 1)]))

        first_w2 = []
        for u, (lo, hi) in enumerate(FIRST_CUTS):
            first_w2.append(work.tile([P, PACK, hi - lo], F32, name="first_w2_%d" % u))
            nc.sync.dma_start(out=first_w2[u][:], in_=w2[0:PASS, lo:hi].rearrange("(p j) c -> p j c", j=PACK))
        nc.sync.dma_start(pos_t[1][:], pos2)
        load_w1(1)
        load_w1_scales(1)
        load_w2(1, 0)
        nc.sync.dma_start(pos_t[2][:], pos3)
        load_w2(0, 1)
        load_w2(1, 1)
        for a in range(2):
            load_rows(("w3", a), w3[a * PASS:(a + 1) * PASS, :])
        for q in range(4):
            nc.sync.dma_start(out=w4_sc[QUAD * q: QUAD * q + 8, :].bitcast(I32),
                              in_=w4_scales[:, 4 * q: 4 * q + 4, :].bitcast(I32))

        codes, scales, woven = {}, {}, {}

        def weave_weight(key, copies):
            if key in LATE_W3:
                woven[key] = work.tile([P, PACK * BANK], BF16, name="bottle_rows", bufs=ROW_BUFS["bottle"], align_bytes=64)
            else:
                woven[key] = work.tile([P, PACK * BANK], BF16, name="woven", bufs=3, align_bytes=64)
            if key[0] == "w2":
                dst = woven[key][:].rearrange("p (t m j) -> p m j t", t=PACK, j=PACK)
            else:
                dst = woven[key][:].rearrange("p (m t j) -> p m j t", t=PACK, j=PACK)
            if key == ("w2", 0, 0):
                for u, (lo, hi) in enumerate(FIRST_CUTS):
                    nc.vector.tensor_copy(out=dst[:, lo // PACK:hi // PACK], in_=first_w2[u][:].rearrange("p j (m t) -> p m j t", t=PACK))
                return
            src = raw[key][:].rearrange("p j (m t) -> p m j t", t=PACK)
            share = P // len(copies)
            for i, copy in enumerate(copies):
                copy(out=dst[:, i * share:(i + 1) * share], in_=src[:, i * share:(i + 1) * share])

        def quantize_weight(key):
            name = "_".join(str(x) for x in key)
            if key not in codes:
                codes[key] = held("codes_" + name, [P, BANK], U32)[:]
            scales[key] = held("scales_" + name, [P, BANK], U8)
            nc.vector.quantize_mx(out=codes[key].bitcast(FP8X4), scales=scales[key][:], in_=woven[key][:])

        on_vector = [nc.vector.tensor_copy]
        on_scalar = [nc.scalar.copy] * 2

        rows = {}

        def first_stage(kind, i, h):
            b, t = divmod(i, PACK)
            if (kind, i) not in rows:
                rows[kind, i] = work.tile([P, S], F32, name=kind + "_rows", bufs=ROW_BUFS[kind], align_bytes=64)
            acc = psum.tile([P, BANK], F32, name="acc")
            profiles = slice(h * BANK, (h + 1) * BANK)
            piece = int(i * P >= FIRST)
            at = i * P - w1_cols[piece].start
            for a in range(2):
                if kind == "dish":
                    lhs, lhs_sc = w1[piece][:, a, 2 * at: 2 * (at + P)].bitcast(FP4X4), w1_sc[piece][:, a, at:at + P]
                else:
                    lhs, lhs_sc = codes["w2", a, b][:, t * P:(t + 1) * P].bitcast(FP8X4), scales["w2", a, b][:, t * P:(t + 1) * P]
                nc.tensor.matmul_mx(out=acc[:], lhsT=lhs, lhsT_scale=lhs_sc,
                                    rhs=v[a][h].bitcast(FP8X4), rhs_scale=v_sc[:, a, profiles],
                                    start=(a == 0), stop=(a == 1))
            nc.scalar.copy(out=rows[kind, i][:, profiles], in_=acc[:])

        parts = {"0": (0, 0, M), "1a": (1, 0, HALF), "1b": (1, HALF, M)}
        low = {}
        for part in parts:
            if part == "1a":
                low[part] = late.tile([P, PACK, HALF], F32, name="low1a", align_bytes=64, offset=WOVEN - 64)
            else:
                low[part] = work.tile([P, PACK, parts[part][2] - parts[part][1]], F32, name="low" + part, align_bytes=64)
        z = {}

        def dish(i):
            b, t = divmod(i, PACK)
            if i >= HEAD_TILES:
                first_stage("dish", i, 0)
            first_stage("dish", i, 1)
            starter = work.tile([P, M], F32, name="starter", bufs=ROW_TILES)
            nc.scalar.activation(out=starter[:], in_=rows["dish", i][:].indirect(pos_t[0][:]), func=ACT.Sigmoid)
            if i == ROW_TILES - 1:
                main = late.tile([P, M], F32, name="last_main", align_bytes=64, offset=6 * WOVEN)
            else:
                main = work.tile([P, M], F32, name="main", bufs=3)
            nc.vector.tensor_copy(out=main[:], in_=rows["dish", i][:].indirect(pos_t[1][:]))
            picks[i] = (starter, main)

        picks = {}

        def least(i):
            b, t = divmod(i, PACK)
            starter, main = picks[i]
            nc.vector.tensor_tensor(out=starter[:], in0=starter[:], in1=main[:], op=ALU.min)
            for part in parts:
                if parts[part][0] == b:
                    nc.sync.dma_start(out=low[part][QUAD * t: QUAD * (t + 1), :, :], in_=starter[:, parts[part][1]:parts[part][2]])

        def times_bottle(part, t):
            b, lo, hi = parts[part]
            if part not in z:
                z[part] = work.tile([P, PACK, hi - lo], F32, name=ZNAME[part], align_bytes=64)
            nc.vector.tensor_tensor(out=z[part][:, t, :],
                                    in0=rows["bottle", PACK * b + t][:].indirect(pos_t[2][:, lo // 16: hi // 16]),
                                    in1=low[part][:, t, :], op=ALU.mult)

        def bottle(i):
            for h in range(2):
                first_stage("bottle", i, h)
            times_bottle(("0", "1a")[i // PACK], i % PACK)

        z_codes, z_scales, z_woven = {}, {}, {}

        def weave_z(b, h, copy):
            src = z["0"][:, :, h * HALF:(h + 1) * HALF] if b == 0 else z[("1a", "1b")[h]][:]
            if b == 0:
                z_woven[b, h] = late.tile([P, PACK * HALF], BF16, name="z_woven0%d" % h, align_bytes=64, offset=h * WOVEN)
            else:
                z_woven[b, h] = work.tile([P, PACK * HALF], BF16, name="z_woven%d%d" % (b, h), align_bytes=64)
            copy(out=z_woven[b, h][:].rearrange("p (c i t) -> p c t i", i=4, t=PACK),
                 in_=src.rearrange("p t (c i) -> p c t i", i=4))

        def quantize_z(b, h):
            if (b, h) not in z_codes:
                z_codes[b, h] = held("z_codes%d%d" % (b, h), [P, HALF], U32)[:]
            z_scales[b, h] = held("z_scales%d%d" % (b, h), [P, HALF], U8)
            nc.vector.quantize_mx(out=z_codes[b, h].bitcast(FP8X4), scales=z_scales[b, h][:], in_=z_woven[b, h][:])

        gather_words(0, 0)
        idle = psum.tile([P, BANK], F32, name="acc")
        for n in range(WARM_PASSES):
            nc.tensor.matmul_mx(out=idle[:], lhsT=v[0][0][:, :P].bitcast(FP8X4), lhsT_scale=picked_sc[:, :P],
                                rhs=v[0][0].bitcast(FP8X4), rhs_scale=picked_sc[:, :BANK],
                                start=(n == 0), stop=(n == WARM_PASSES - 1))
        gather_words(0, 1)
        gather_words(1, 0)
        for i in range(HEAD_TILES):
            first_stage("dish", i, 0)
        gather_words(1, 1)
        w2_keys = [("w2", a, b) for b in range(2) for a in range(2)] + EARLY_W3
        for i in range(ROW_TILES):
            if i < len(w2_keys):
                weave_weight(w2_keys[i], on_scalar if i in ON_SCALAR else on_vector)
            dish(i)
            if i > 0:
                least(i - 1)
            if i < len(w2_keys):
                quantize_weight(w2_keys[i])
        least(ROW_TILES - 1)

        w4 = late.tile([P, 2, N], I32, name="w4", align_bytes=64, offset=6 * WOVEN)
        nc.sync.dma_start(out=w4[:], in_=w4_words.rearrange("a p c i -> p a (c i)").bitcast(I32))
        for i in range(PACK):
            bottle(i)
        house_t = work.tile([P, N // P, M], F32, name="low0", align_bytes=64)
        nc.sync.dma_start(out=house_t[:], in_=house.rearrange("(j p) m -> p j m", p=P))
        for i in range(PACK, ROW_TILES):
            bottle(i)
        for key in LATE_W3:
            weave_weight(key, on_scalar)
        late_codes = late.tile([P, 3 * BANK], U32, name="late_codes", align_bytes=64, offset=2 * WOVEN)
        z_codes[0, 0], z_codes[0, 1] = late_codes[:, :HALF], late_codes[:, HALF:BANK]
        for key in LATE_W3:
            codes[key] = late_codes[:, (1 + key[1]) * BANK:(2 + key[1]) * BANK]

        banks = {}

        def second_stage(kind, j, a, h):
            if (kind, j) not in banks:
                banks[kind, j] = psum.tile([P, M], F32, name="acc")
            cols = slice(j * P, (j + 1) * P)
            menus = slice(h * HALF, (h + 1) * HALF)
            if kind == "e":
                lhs, lhs_sc = codes["w3", a][:, cols], scales["w3", a][:, cols]
            else:
                lhs, lhs_sc = w4[:, a, cols], w4_sc[4 * a:, cols]
            nc.tensor.matmul_mx(out=banks[kind, j][:, menus], lhsT=lhs.bitcast(FP8X4), lhsT_scale=lhs_sc,
                                rhs=z_codes[a, h].bitcast(FP8X4), rhs_scale=z_scales[a, h][:],
                                start=(a == 0), stop=(a == 1))

        def finish(j, h, change, engine):
            menus = slice(h * HALF, (h + 1) * HALF)
            engine.tensor_tensor(out=change[:], in0=change[:], in1=house_t[:, j, menus], op=ALU.add)
            nc.sync.dma_start(out=out[j * P:(j + 1) * P, menus], in_=change[:])

        def epilogue(h, engines):
            menus = slice(h * HALF, (h + 1) * HALF)
            last = None
            for j in range(N // P):
                change = work.tile([P, HALF], F32, name="change", bufs=8)
                nc.scalar.activation(out=change[:], in_=banks["e", j][:, menus], func=ACT.Sigmoid)
                nc.vector.tensor_tensor(out=change[:], in0=banks["d", j][:, menus], in1=change[:], op=ALU.mult)
                if last is not None:
                    finish(*last)
                last = (j, h, change, engines[j])
            finish(*last)

        weave_z(0, 0, nc.vector.tensor_copy)
        weave_z(1, 0, nc.scalar.copy)
        weave_z(0, 1, nc.scalar.copy)
        quantize_weight(("w3", 0))
        quantize_z(0, 0)
        for t in range(PACK):
            if t == PACK - 1:
                quantize_weight(("w3", 1))
            times_bottle("1b", t)
        quantize_z(1, 0)
        weave_z(1, 1, nc.vector.tensor_copy)
        quantize_z(0, 1)
        quantize_z(1, 1)
        for a in range(2):
            for j in range(N // P):
                for kind in "ed":
                    second_stage(kind, j, a, 0)
        epilogue(0, [nc.vector] * 4)
        for j in range(N // P):
            for kind in "ed":
                for a in range(2):
                    second_stage(kind, j, a, 1)
        epilogue(1, [nc.vector] * 4)
